import numpy as np
import ml_dtypes


def mxq(x, axis, fmt="e4m3"):
    dtype, down = {"e4m3": (ml_dtypes.float8_e4m3fn, 7), "e5m2": (ml_dtypes.float8_e5m2, 14)}[fmt]
    v = np.moveaxis(np.asarray(x, np.float32).astype(ml_dtypes.bfloat16).astype(np.float64), axis, -1)
    blocks = v.reshape(v.shape[:-1] + (-1, 32))
    amax = np.abs(blocks).max(-1, keepdims=True)
    byte = np.maximum(np.where(amax > 0, np.frexp(amax)[1] - 1 + 127, 0) - down, 1)
    scale = np.exp2(byte - 127.0)
    codes = (blocks / scale).astype(np.float32).astype(dtype).astype(np.float64)
    return np.moveaxis((codes * scale).reshape(v.shape), -1, axis)


WIDE = False


def mx_kscale(k):
    if not WIDE:
        return np.ones(k)
    levels = np.array([10, -10, 5, -5, 0])
    if k % 512:
        return np.exp2(np.random.permutation(np.resize(levels, k // 32))).repeat(32)
    a = np.empty((k // 512, 16))
    for p in range(k // 512):
        a[p, :8] = np.random.permutation(np.resize(levels, 8))
        for g in range(8):
            far = levels[np.abs(levels - a[p, g]) >= 10]
            a[p, g + 8] = far[np.random.randint(len(far))]
    return np.exp2(a.ravel()).repeat(32)


def f64(x):
    return np.asarray(x).astype(np.float64)


def striped(idx):
    return np.tile(idx.reshape(-1, 16).T, (8, 1)).astype(np.uint16)


def unstriped(offs):
    return offs[:16].T.reshape(-1).astype(np.int64)


def pack_weight(w):
    k, n = w.shape
    w = f64(np.asarray(w, np.float32).astype(ml_dtypes.bfloat16)).reshape(k // 32, 32, n)
    amax = np.abs(w).max(1)
    byte = np.clip(np.where(amax > 0, np.frexp(amax)[1] - 1 + 127 - 7, 1), 1, 254)
    scaled = (w * np.exp2(127.0 - byte)[:, None, :]).reshape(k, n).astype(np.float32)
    words = np.ascontiguousarray(scaled.reshape(k // 512, 128, 4, n).transpose(0, 1, 3, 2)).astype(ml_dtypes.float8_e4m3fn).view(np.uint8)
    return words, np.ascontiguousarray(byte.astype(np.uint8).reshape(k // 512, 16, n))


def unpack_weight(words, scales):
    g, p, n, _ = words.shape
    vals = np.ascontiguousarray(words).view(ml_dtypes.float8_e4m3fn).astype(np.float64) * np.repeat(np.exp2(scales.astype(np.float64) - 127.0), 8, axis=1)[..., None]
    return vals.transpose(0, 1, 3, 2).reshape(g * 512, n)


def gelu(v):
    return 0.5 * v * (1.0 + np.tanh(np.sqrt(2.0 / np.pi) * (v + 0.044715 * v**3)))


K, T, S, H, N = 1024, 2048, 1024, 512, 128
P = 2 ** 7


def setup_inputs():
    n = np.random.standard_normal
    s = mx_kscale(K)[:, None]
    u = mx_kscale(H)
    packed_xT = pack_weight(n((K, T)) * s)
    packed_w2 = pack_weight(n((H, N)) / np.sqrt(H) / u[:, None])
    return {
        "x_words": packed_xT[0],
        "x_scales": packed_xT[1],
        "w1": (n((K, H)) / np.sqrt(K) / s * u).astype(np.float32),
        "w2_words": packed_w2[0],
        "w2_scales": packed_w2[1],
        "share": np.tile(np.random.uniform(0.1, 0.9, S), (P, 1)).astype(np.float32),
        "offs": striped(np.random.permutation(T)[:S]),
        "par": striped(np.random.permutation(S)[(S * np.random.uniform(0, 1, S) ** 4).astype(np.int64)]),
    }


def reference(x_words, x_scales, w1, w2_words, w2_scales, share, offs, par):
    xq = unpack_weight(x_words, x_scales)[:, unstriped(offs)]
    h = gelu(mxq(f64(w1), 0, "e4m3").T @ xq)
    z = h + h[:, unstriped(par)] * f64(share)[:1]
    return unpack_weight(w2_words, w2_scales).T @ mxq(z, 0, "e4m3")

@@ -1,0 +1,223 @@
+from contextlib import ExitStack
+
+import concourse.mybir as mybir
+from concourse.masks import make_identity
+
+K, T, S, H, N = 1024, 2048, 1024, 512, 128
+FLOPS = 2 * K * H * S + 2 * H * N * S
+
+F32 = mybir.dt.float32
+BF16 = mybir.dt.bfloat16
+I32 = mybir.dt.int32
+U32 = mybir.dt.uint32
+U16 = mybir.dt.uint16
+U8 = mybir.dt.uint8
+FP8X4 = mybir.dt.float8_e4m3fn_x4
+GELU = mybir.ActivationFunctionType.Gelu_apprx_tanh
+MULT = mybir.AluOpType.mult
+
+P = 128
+PASSES = K // 512
+CHUNKS = H // P
+HALF = S // 2
+QUARTER = S // 4
+
+
+def tile_picked_treeup_gelu_p_kernel(
+    tc, x_words, x_scales, w1, w2_words, w2_scales, share, offs, par, out
+):
+    nc = tc.nc
+    with ExitStack() as ctx:
+        keep = ctx.enter_context(tc.tile_pool(name="keep", bufs=1))
+        psum = ctx.enter_context(tc.psum_pool(name="psum", bufs=1))
+
+        offs_sb = keep.tile([P, S // 16], U16, name="offs_sb")
+        par_sb = keep.tile([P, S // 16], U16, name="par_sb")
+        x_table = [keep.tile([P, T], U32, name="x_table%d" % g) for g in range(PASSES)]
+        xs_table = keep.tile([P, T], U8, name="xs_table")
+        w1_raw = [[keep.tile([P, 4, P], F32, name="w1_raw%d_%d" % (c, g)) for g in range(PASSES)] for c in range(CHUNKS)]
+        share_sb = [keep.tile([P, HALF], F32, name="share%d" % a) for a in range(2)]
+        w2_codes = keep.tile([P, N], U32, name="w2_codes", align_bytes=64)
+        w2_plane = keep.tile([P, N], U8, name="w2_plane", align_bytes=64)
+        ident = keep.tile([P, P], F32, name="ident")
+
+        nc.gpsimd.memset(xs_table[:].bitcast(I32), 0)
+        nc.sync.dma_start(offs_sb[:], offs)
+        nc.sync.dma_start(par_sb[:], par)
+        for q in range(4):
+            nc.sync.dma_start(out=xs_table[32 * q : 32 * q + 8, :].bitcast(I32), in_=x_scales[:, 4 * q : 4 * q + 4, :].bitcast(I32))
+
+        def load_x(g):
+            nc.sync.dma_start(out=x_table[g][:].bitcast(I32), in_=x_words[g].rearrange("p n t -> p (n t)").bitcast(I32))
+
+        def load_w1(c):
+            for g in range(PASSES):
+                nc.sync.dma_start(
+                    out=w1_raw[c][g][:],
+                    in_=w1[512 * g : 512 * (g + 1), P * c : P * (c + 1)].rearrange("(p r) m -> p r m", r=4),
+                )
+
+        load_x(0)
+        load_w1(0)
+        load_x(1)
+        load_w1(1)
+        nc.sync.dma_start(out=share_sb[0][:], in_=share[:, 0:HALF])
+        nc.sync.dma_start(out=share_sb[1][:], in_=share[:, HALF:S])
+        load_w1(2)
+        load_w1(3)
+        nc.gpsimd.memset(w2_plane[:], 0)
+        make_identity(nc, ident[:])
+        nc.sync.dma_start(out=w2_codes[:].bitcast(I32), in_=w2_words[0].rearrange("p n t -> p (n t)").bitcast(I32))
+        for q in range(4):
+            nc.sync.dma_start(out=w2_plane[32 * q : 32 * q + 4, :].bitcast(I32), in_=w2_scales[0, 4 * q : 4 * q + 4, :].bitcast(I32))
+
+        x_plane = keep.tile([P, S], U8, name="x_plane", align_bytes=64)
+        x_codes = [[keep.tile([P, HALF], U32, name="x_codes%d_%d" % (g, a), align_bytes=64) for a in range(2)] for g in range(PASSES)]
+
+        def gather_x(g, a):
+            nc.vector.tensor_copy(x_codes[g][a][:], x_table[g][:].indirect(offs_sb[:, 32 * a : 32 * (a + 1)]))
+
+        w1_bf = [[keep.tile([P, P, 4], BF16, name="w1_bf%d_%d" % (c, g), tag="stage%d_%d" % (c, g), align_bytes=64) for g in range(PASSES)] for c in range(CHUNKS)]
+        w1_codes = [[keep.tile([P, P], U32, name="w1_codes%d_%d" % (c, g), align_bytes=64) for g in range(PASSES)] for c in range(CHUNKS)]
+        w1_plane = [[keep.tile([P, P], U8, name="w1_plane%d_%d" % (c, g), align_bytes=64) for g in range(PASSES)] for c in range(CHUNKS)]
+
+        def cast_w1(c, g):
+            dst = w1_bf[c][g][:].rearrange("p (m i) r -> p m r i", i=4)
+            src = w1_raw[c][g][:].rearrange("p r (m i) -> p m r i", i=4)
+            if c in (0, 2):
+                nc.scalar.copy(dst, src)
+            else:
+                nc.vector.tensor_copy(dst, src)
+
+        def quantize_w1(c, g):
+            nc.vector.quantize_mx(
+                out=w1_codes[c][g][:].bitcast(FP8X4), scales=w1_plane[c][g][:], in_=w1_bf[c][g][:].rearrange("p m r -> p (m r)")
+            )
+
+        h = [keep.tile([P, S], F32, name="h%d" % c) for c in range(CHUNKS)]
+
+        def first_layer(c):
+            banks = [psum.tile([P, HALF], F32, name="pre", tag="pre", bufs=4) for a in range(2)]
+            for g in range(PASSES):
+                for a in range(2):
+                    nc.tensor.matmul_mx(
+                        banks[a][:],
+                        lhsT=w1_codes[c][g][:].bitcast(FP8X4),
+                        lhsT_scale=w1_plane[c][g][:],
+                        rhs=x_codes[g][a][:].bitcast(FP8X4),
+                        rhs_scale=x_plane[4 * g : P, HALF * a : HALF * (a + 1)],
+                        start=(g == 0),
+                        stop=(g == PASSES - 1),
+                    )
+            for a in range(2):
+                nc.scalar.activation(h[c][:, HALF * a : HALF * (a + 1)], banks[a][:], GELU)
+
+        z_rows = [keep.tile([P, 2, 2, P, 2], BF16, name="z_rows%d" % q) for q in range(4)]
+
+        def mix(c, j0, width, slot):
+            blocks = width // P
+            taken = keep.tile([P, width], F32, name="taken", tag=slot, align_bytes=64)
+            a = j0 // HALF
+            nc.vector.tensor_tensor(
+                taken[:],
+                h[c][:].indirect(par_sb[:, j0 // 16 : (j0 + width) // 16]),
+                share_sb[a][:, j0 - HALF * a : j0 - HALF * a + width],
+                MULT,
+            )
+            bank = psum.tile([P, blocks, P], F32, name="zt", tag="zt", bufs=2)
+            for b in range(blocks):
+                nc.tensor.matmul(
+                    bank[:, b, :], lhsT=h[c][:, j0 + P * b : j0 + P * (b + 1)], rhs=ident[:], is_transpose=True, start=(b == 0), stop=False
+                )
+            for b in range(blocks):
+                nc.tensor.matmul(
+                    bank[:, b, :], lhsT=taken[:, P * b : P * (b + 1)], rhs=ident[:], is_transpose=True, start=False, stop=(b == blocks - 1)
+                )
+            for k in range(width // QUARTER):
+                q = j0 // QUARTER + k
+                nc.scalar.copy(
+                    z_rows[q][:, :, :, 32 * c : 32 * (c + 1), :],
+                    bank[:, 2 * k : 2 * k + 2, :].rearrange("j b (p u e) -> j b u p e", u=2, e=2),
+                )
+
+        z_bf = [keep.tile([P, QUARTER * 4], BF16, name="z_bf%d" % q, align_bytes=64) for q in range(4)]
+        acc = {}
+
+        def turn(q):
+            words = z_rows[q][:].rearrange("j b u p e -> j (b u p e)").bitcast(F32)
+            bank = psum.tile([P, 2, 2, P], F32, name="zw", tag="zw", bufs=2)
+            for b in range(2):
+                for u in range(2):
+                    nc.tensor.transpose(bank[:, b, u, :], words[:, P * (2 * b + u) : P * (2 * b + u + 1)], ident[:])
+            dst = z_bf[q][:].bitcast(F32).rearrange("p (b j u) -> p b j u", b=2, u=2)
+            src = bank[:].rearrange("p b u j -> p b j u")
+            if q in (0, 1, 3):
+                nc.scalar.copy(dst, src)
+            else:
+                nc.vector.tensor_copy(dst, src)
+
+        def second_layer(q):
+            z_codes = keep.tile([P, QUARTER], U32, name="z_codes%d" % q, align_bytes=64)
+            z_plane = keep.tile([P, QUARTER], U8, name="z_plane%d" % q, align_bytes=64)
+            nc.vector.quantize_mx(out=z_codes[:].bitcast(FP8X4), scales=z_plane[:], in_=z_bf[q][:])
+            acc[q] = psum.tile([P, QUARTER], F32, name="acc", tag="pre", bufs=4)
+            nc.tensor.matmul_mx(
+                acc[q][:],
+                lhsT=w2_codes[:].bitcast(FP8X4),
+                lhsT_scale=w2_plane[:],
+                rhs=z_codes[:].bitcast(FP8X4),
+                rhs_scale=z_plane[:],
+                start=True,
+                stop=True,
+            )
+
+        def finish(q):
+            res = keep.tile([P, QUARTER], F32, name="res%d" % q)
+            if q in (0, 1):
+                nc.scalar.copy(res[:], acc[q][:])
+            else:
+                nc.vector.tensor_copy(res[:], acc[q][:])
+            nc.sync.dma_start(out=out[:, QUARTER * q : QUARTER * (q + 1)], in_=res[:])
+
+        nc.vector.tensor_copy(x_plane[:], xs_table[:].indirect(offs_sb[:]))
+        gather_x(0, 0)
+        gather_x(0, 1)
+        for g in range(PASSES):
+            cast_w1(0, g)
+            quantize_w1(0, g)
+        gather_x(1, 0)
+        gather_x(1, 1)
+        first_layer(0)
+
+        def prepare(c):
+            for g in range(PASSES):
+                cast_w1(c, g)
+            for g in range(PASSES):
+                quantize_w1(c, g)
+            first_layer(c)
+
+        prepare(1)
+        prepare(2)
+        mix(0, 0, HALF, "stage1_1")
+        mix(0, HALF, HALF, "taken0")
+        prepare(3)
+        mix(1, 0, HALF, "stage2_1")
+        mix(1, HALF, HALF, "stage3_1")
+        mix(2, 0, HALF, "taken1")
+        mix(3, 0, QUARTER, "taken2")
+        mix(3, QUARTER, QUARTER, "taken3")
+        turn(0)
+        turn(1)
+        mix(2, HALF, HALF, "taken2")
+        second_layer(0)
+        second_layer(1)
+        mix(3, 2 * QUARTER, QUARTER, "taken4")
+        mix(3, 3 * QUARTER, QUARTER, "taken5")
+        finish(0)
+        finish(1)
+        turn(2)
+        turn(3)
+        second_layer(2)
+        second_layer(3)
+        finish(2)
+        finish(3)

@@ -21,6 +21,8 @@ PASSES = K // 512
 CHUNKS = H // P
 HALF = S // 2
 QUARTER = S // 4
+STRETCHES = ((0, 512), (512, 256), (768, 128), (896, 128))
+PIECES = ((0, 256), (256, 256), (512, 256), (768, 128), (896, 128))
 
 
 def tile_picked_treeup_gelu_p_kernel(
@@ -35,8 +37,9 @@ def tile_picked_treeup_gelu_p_kernel(
         par_sb = keep.tile([P, S // 16], U16, name="par_sb")
         x_table = [keep.tile([P, T], U32, name="x_table%d" % g) for g in range(PASSES)]
         xs_table = keep.tile([P, T], U8, name="xs_table")
-        w1_raw = [[keep.tile([P, 4, P], F32, name="w1_raw%d_%d" % (c, g)) for g in range(PASSES)] for c in range(CHUNKS)]
-        share_sb = [keep.tile([P, HALF], F32, name="share%d" % a) for a in range(2)]
+        spans = ((0, 1), (1, 3), (3, 4))
+        w1_raw = [[keep.tile([P, 4, P * (hi - lo)], F32, name="w1_raw%d_%d" % (lo, g), tag="raw%d_%d" % (lo, g)) for g in range(PASSES)] for lo, hi in spans]
+        share_sb = [keep.tile([P, HALF], F32, name="share%d" % a, tag="share%d" % a, align_bytes=64) for a in range(2)]
         w2_codes = keep.tile([P, N], U32, name="w2_codes", align_bytes=64)
         w2_plane = keep.tile([P, N], U8, name="w2_plane", align_bytes=64)
         ident = keep.tile([P, P], F32, name="ident")
@@ -50,31 +53,34 @@ def tile_picked_treeup_gelu_p_kernel(
         def load_x(g):
             nc.sync.dma_start(out=x_table[g][:].bitcast(I32), in_=x_words[g].rearrange("p n t -> p (n t)").bitcast(I32))
 
-        def load_w1(c):
-            for g in range(PASSES):
-                nc.sync.dma_start(
-                    out=w1_raw[c][g][:],
-                    in_=w1[512 * g : 512 * (g + 1), P * c : P * (c + 1)].rearrange("(p r) m -> p r m", r=4),
-                )
+        def load_w1(s, g):
+            lo, hi = spans[s]
+            nc.sync.dma_start(
+                out=w1_raw[s][g][:],
+                in_=w1[512 * g : 512 * (g + 1), P * lo : P * hi].rearrange("(p r) m -> p r m", r=4),
+            )
 
         load_x(0)
-        load_w1(0)
+        load_w1(0, 0)
+        load_w1(0, 1)
         load_x(1)
-        load_w1(1)
+        load_w1(1, 0)
         nc.sync.dma_start(out=share_sb[0][:], in_=share[:, 0:HALF])
+        load_w1(1, 1)
         nc.sync.dma_start(out=share_sb[1][:], in_=share[:, HALF:S])
-        load_w1(2)
-        load_w1(3)
+        load_w1(2, 0)
+        load_w1(2, 1)
         nc.gpsimd.memset(w2_plane[:], 0)
         make_identity(nc, ident[:])
-        nc.sync.dma_start(out=w2_codes[:].bitcast(I32), in_=w2_words[0].rearrange("p n t -> p (n t)").bitcast(I32))
+        nc.gpsimd.dma_start(out=w2_codes[:].bitcast(I32), in_=w2_words[0].rearrange("p n t -> p (n t)").bitcast(I32))
         for q in range(4):
-            nc.sync.dma_start(out=w2_plane[32 * q : 32 * q + 4, :].bitcast(I32), in_=w2_scales[0, 4 * q : 4 * q + 4, :].bitcast(I32))
+            nc.gpsimd.dma_start(out=w2_plane[32 * q : 32 * q + 4, :].bitcast(I32), in_=w2_scales[0, 4 * q : 4 * q + 4, :].bitcast(I32))
 
         x_plane = keep.tile([P, S], U8, name="x_plane", align_bytes=64)
-        x_codes = [[keep.tile([P, HALF], U32, name="x_codes%d_%d" % (g, a), align_bytes=64) for a in range(2)] for g in range(PASSES)]
+        x_codes = [{}, {}]
 
-        def gather_x(g, a):
+        def gather_x(g, a, slot):
+            x_codes[g][a] = keep.tile([P, HALF], U32, name="x_codes", tag=slot, align_bytes=64)
             nc.vector.tensor_copy(x_codes[g][a][:], x_table[g][:].indirect(offs_sb[:, 32 * a : 32 * (a + 1)]))
 
         w1_bf = [[keep.tile([P, P, 4], BF16, name="w1_bf%d_%d" % (c, g), tag="stage%d_%d" % (c, g), align_bytes=64) for g in range(PASSES)] for c in range(CHUNKS)]
@@ -83,8 +89,10 @@ def tile_picked_treeup_gelu_p_kernel(
 
         def cast_w1(c, g):
             dst = w1_bf[c][g][:].rearrange("p (m i) r -> p m r i", i=4)
-            src = w1_raw[c][g][:].rearrange("p r (m i) -> p m r i", i=4)
-            if c in (0, 2):
+            s = [k for k in range(3) if spans[k][0] <= c < spans[k][1]][0]
+            m0 = P * (c - spans[s][0])
+            src = w1_raw[s][g][:, :, m0 : m0 + P].rearrange("p r (m i) -> p m r i", i=4)
+            if (c, g) in ((0, 0), (0, 1), (1, 0), (2, 0), (2, 1), (3, 0), (3, 1)):
                 nc.scalar.copy(dst, src)
             else:
                 nc.vector.tensor_copy(dst, src)
@@ -94,10 +102,11 @@ def tile_picked_treeup_gelu_p_kernel(
                 out=w1_codes[c][g][:].bitcast(FP8X4), scales=w1_plane[c][g][:], in_=w1_bf[c][g][:].rearrange("p m r -> p (m r)")
             )
 
-        h = [keep.tile([P, S], F32, name="h%d" % c) for c in range(CHUNKS)]
+        h = {}
 
-        def first_layer(c):
-            banks = [psum.tile([P, HALF], F32, name="pre", tag="pre", bufs=4) for a in range(2)]
+        def first_layer(c, slot):
+            h[c] = keep.tile([P, S], F32, name="h%d" % c, tag=slot)
+            banks = [psum.tile([P, HALF], F32, name="pre", tag="pre", bufs=3) for a in range(2)]
             for g in range(PASSES):
                 for a in range(2):
                     nc.tensor.matmul_mx(
@@ -112,11 +121,13 @@ def tile_picked_treeup_gelu_p_kernel(
             for a in range(2):
                 nc.scalar.activation(h[c][:, HALF * a : HALF * (a + 1)], banks[a][:], GELU)
 
-        z_rows = [keep.tile([P, 2, 2, P, 2], BF16, name="z_rows%d" % q) for q in range(4)]
+        z_rows = [keep.tile([P, w // P, 2, P, 2], BF16, name="z_rows%d" % q) for q, (j, w) in enumerate(STRETCHES)]
 
-        def mix(c, j0, width, slot):
+        def room(slot, width):
+            return keep.tile([P, width], F32, name="taken", tag=slot, align_bytes=64)
+
+        def mix(c, j0, width, taken):
             blocks = width // P
-            taken = keep.tile([P, width], F32, name="taken", tag=slot, align_bytes=64)
             a = j0 // HALF
             nc.vector.tensor_tensor(
                 taken[:],
@@ -124,7 +135,7 @@ def tile_picked_treeup_gelu_p_kernel(
                 share_sb[a][:, j0 - HALF * a : j0 - HALF * a + width],
                 MULT,
             )
-            bank = psum.tile([P, blocks, P], F32, name="zt", tag="zt", bufs=2)
+            bank = psum.tile([P, blocks, P], F32, name="zt", tag="zt", bufs=3)
             for b in range(blocks):
                 nc.tensor.matmul(
                     bank[:, b, :], lhsT=h[c][:, j0 + P * b : j0 + P * (b + 1)], rhs=ident[:], is_transpose=True, start=(b == 0), stop=False
@@ -133,34 +144,42 @@ def tile_picked_treeup_gelu_p_kernel(
                 nc.tensor.matmul(
                     bank[:, b, :], lhsT=taken[:, P * b : P * (b + 1)], rhs=ident[:], is_transpose=True, start=False, stop=(b == blocks - 1)
                 )
-            for k in range(width // QUARTER):
-                q = j0 // QUARTER + k
-                nc.scalar.copy(
-                    z_rows[q][:, :, :, 32 * c : 32 * (c + 1), :],
-                    bank[:, 2 * k : 2 * k + 2, :].rearrange("j b (p u e) -> j b u p e", u=2, e=2),
-                )
+            for q, (j, w) in enumerate(STRETCHES):
+                if j0 <= j < j0 + width:
+                    b0 = (j - j0) // P
+                    nc.scalar.copy(
+                        z_rows[q][:, :, :, 32 * c : 32 * (c + 1), :],
+                        bank[:, b0 : b0 + w // P, :].rearrange("j b (p u e) -> j b u p e", u=2, e=2),
+                    )
 
-        z_bf = [keep.tile([P, QUARTER * 4], BF16, name="z_bf%d" % q, align_bytes=64) for q in range(4)]
+        z_bf = {}
         acc = {}
 
-        def turn(q):
-            words = z_rows[q][:].rearrange("j b u p e -> j (b u p e)").bitcast(F32)
-            bank = psum.tile([P, 2, 2, P], F32, name="zw", tag="zw", bufs=2)
-            for b in range(2):
+        def turn(q, on_scalar, slot):
+            j, w = PIECES[q]
+            s = [k for k, (j1, w1s) in enumerate(STRETCHES) if j1 <= j < j1 + w1s][0]
+            b0 = (j - STRETCHES[s][0]) // P
+            words = z_rows[s][:].rearrange("j b u p e -> j (b u p e)").bitcast(F32)
+            blocks = w // P
+            bank = psum.tile([P, blocks, 2, P], F32, name="zw", tag="zw", bufs=2)
+            for b in range(blocks):
                 for u in range(2):
-                    nc.tensor.transpose(bank[:, b, u, :], words[:, P * (2 * b + u) : P * (2 * b + u + 1)], ident[:])
-            dst = z_bf[q][:].bitcast(F32).rearrange("p (b j u) -> p b j u", b=2, u=2)
+                    m0 = P * (2 * (b0 + b) + u)
+                    nc.tensor.transpose(bank[:, b, u, :], words[:, m0 : m0 + P], ident[:])
+            z_bf[q] = keep.tile([P, 4 * w], BF16, name="z_bf", tag=slot, align_bytes=64)
+            dst = z_bf[q][:].bitcast(F32).rearrange("p (b j u) -> p b j u", b=blocks, u=2)
             src = bank[:].rearrange("p b u j -> p b j u")
-            if q in (0, 1, 3):
+            if on_scalar:
                 nc.scalar.copy(dst, src)
             else:
                 nc.vector.tensor_copy(dst, src)
 
         def second_layer(q):
-            z_codes = keep.tile([P, QUARTER], U32, name="z_codes%d" % q, align_bytes=64)
-            z_plane = keep.tile([P, QUARTER], U8, name="z_plane%d" % q, align_bytes=64)
+            w = PIECES[q][1]
+            z_codes = keep.tile([P, w], U32, name="z_codes%d" % q, align_bytes=64)
+            z_plane = keep.tile([P, w], U8, name="z_plane%d" % q, align_bytes=64)
             nc.vector.quantize_mx(out=z_codes[:].bitcast(FP8X4), scales=z_plane[:], in_=z_bf[q][:])
-            acc[q] = psum.tile([P, QUARTER], F32, name="acc", tag="pre", bufs=4)
+            acc[q] = psum.tile([P, w], F32, name="acc", tag="pre", bufs=3)
             nc.tensor.matmul_mx(
                 acc[q][:],
                 lhsT=w2_codes[:].bitcast(FP8X4),
@@ -171,53 +190,62 @@ def tile_picked_treeup_gelu_p_kernel(
                 stop=True,
             )
 
-        def finish(q):
-            res = keep.tile([P, QUARTER], F32, name="res%d" % q)
-            if q in (0, 1):
+        def finish(q, on_scalar):
+            j, w = PIECES[q]
+            res = keep.tile([P, w], F32, name="res%d" % q)
+            if on_scalar:
                 nc.scalar.copy(res[:], acc[q][:])
             else:
                 nc.vector.tensor_copy(res[:], acc[q][:])
-            nc.sync.dma_start(out=out[:, QUARTER * q : QUARTER * (q + 1)], in_=res[:])
+            nc.sync.dma_start(out=out[:, j : j + w], in_=res[:])
 
         nc.vector.tensor_copy(x_plane[:], xs_table[:].indirect(offs_sb[:]))
-        gather_x(0, 0)
-        gather_x(0, 1)
+        gather_x(0, 0, "x00")
+        gather_x(0, 1, "x01")
         for g in range(PASSES):
             cast_w1(0, g)
             quantize_w1(0, g)
-        gather_x(1, 0)
-        gather_x(1, 1)
-        first_layer(0)
-
-        def prepare(c):
-            for g in range(PASSES):
-                cast_w1(c, g)
-            for g in range(PASSES):
-                quantize_w1(c, g)
-            first_layer(c)
-
-        prepare(1)
-        prepare(2)
-        mix(0, 0, HALF, "stage1_1")
-        mix(0, HALF, HALF, "taken0")
-        prepare(3)
-        mix(1, 0, HALF, "stage2_1")
-        mix(1, HALF, HALF, "stage3_1")
-        mix(2, 0, HALF, "taken1")
-        mix(3, 0, QUARTER, "taken2")
-        mix(3, QUARTER, QUARTER, "taken3")
-        turn(0)
-        turn(1)
-        mix(2, HALF, HALF, "taken2")
+        gather_x(1, 0, "x10")
+        gather_x(1, 1, "x11")
+        cast_w1(1, 0)
+        cast_w1(2, 0)
+        first_layer(0, "raw1_0")
+        quantize_w1(1, 0)
+        cast_w1(1, 1)
+        quantize_w1(2, 0)
+        quantize_w1(1, 1)
+        cast_w1(2, 1)
+        first_layer(1, "h1")
+        for g in range(PASSES):
+            cast_w1(3, g)
+        mix(0, 0, HALF, room("stage1_1", HALF))
+        quantize_w1(2, 1)
+        first_layer(2, "h2")
+        mix(0, HALF, HALF, room("stage2_1", HALF))
+        mix(1, 0, HALF, room("taken0", HALF))
+        for g in range(PASSES):
+            quantize_w1(3, g)
+        first_layer(3, "h3")
+        mix(1, HALF, HALF, room("stage3_1", HALF))
+        mix(2, 0, HALF, room("taken1", HALF))
+        mix(3, 0, HALF, room("taken2", HALF))
+        last = room("share0", S)
+        mix(2, HALF, HALF, last[:, 0:HALF])
+        turn(0, True, "z0")
+        mix(3, 512, 256, last[:, 512:768])
+        mix(3, 768, 128, last[:, 768:896])
+        mix(3, 896, 128, last[:, 896:1024])
+        turn(1, False, "share1")
         second_layer(0)
+        turn(2, True, "z2")
         second_layer(1)
-        mix(3, 2 * QUARTER, QUARTER, "taken4")
-        mix(3, 3 * QUARTER, QUARTER, "taken5")
-        finish(0)
-        finish(1)
-        turn(2)
-        turn(3)
+        turn(3, False, "z3")
+        turn(4, True, "z4")
         second_layer(2)
         second_layer(3)
-        finish(2)
-        finish(3)
+        second_layer(4)
+        finish(0, True)
+        finish(1, True)
+        finish(2, False)
+        finish(3, True)
+        finish(4, False)

@@ -22,6 +22,7 @@ CHUNKS = H // P
 HALF = S // 2
 QUARTER = S // 4
 STRETCHES = ((0, 512), (512, 256), (768, 128), (896, 128))
+RINGS = {"pre": 3, "zt": 3, "zw": 2}
 PIECES = ((0, 256), (256, 256), (512, 256), (768, 128), (896, 128))
 
 
@@ -45,6 +46,10 @@ def tile_picked_treeup_gelu_p_kernel(
         ident = keep.tile([P, P], F32, name="ident")
 
         nc.gpsimd.memset(xs_table[:].bitcast(I32), 0)
+        warm_in = keep.tile([P, 1], F32, name="warm_in")
+        warm_out = keep.tile([P, 1], F32, name="warm_out")
+        nc.vector.memset(warm_in[:], 0.0)
+        nc.scalar.activation(warm_out[:], warm_in[:], GELU)
         nc.sync.dma_start(offs_sb[:], offs)
         nc.sync.dma_start(par_sb[:], par)
         for q in range(4):
@@ -72,9 +77,9 @@ def tile_picked_treeup_gelu_p_kernel(
         load_w1(2, 1)
         nc.gpsimd.memset(w2_plane[:], 0)
         make_identity(nc, ident[:])
-        nc.gpsimd.dma_start(out=w2_codes[:].bitcast(I32), in_=w2_words[0].rearrange("p n t -> p (n t)").bitcast(I32))
+        nc.sync.dma_start(out=w2_codes[:].bitcast(I32), in_=w2_words[0].rearrange("p n t -> p (n t)").bitcast(I32))
         for q in range(4):
-            nc.gpsimd.dma_start(out=w2_plane[32 * q : 32 * q + 4, :].bitcast(I32), in_=w2_scales[0, 4 * q : 4 * q + 4, :].bitcast(I32))
+            nc.sync.dma_start(out=w2_plane[32 * q : 32 * q + 4, :].bitcast(I32), in_=w2_scales[0, 4 * q : 4 * q + 4, :].bitcast(I32))
 
         x_plane = keep.tile([P, S], U8, name="x_plane", align_bytes=64)
         x_codes = [{}, {}]
@@ -126,7 +131,22 @@ def tile_picked_treeup_gelu_p_kernel(
         def room(slot, width):
             return keep.tile([P, width], F32, name="taken", tag=slot, align_bytes=64)
 
-        def mix(c, j0, width, taken):
+        sums = {}
+
+        def begin(c, j0, width, ring):
+            blocks = width // P
+            sums[c, j0] = psum.tile([P, blocks, P], F32, name="zt", tag=ring, bufs=RINGS[ring])
+            for b in range(blocks):
+                nc.tensor.matmul(
+                    sums[c, j0][:, b, :],
+                    lhsT=h[c][:, j0 + P * b : j0 + P * (b + 1)],
+                    rhs=ident[:],
+                    is_transpose=True,
+                    start=(b == 0),
+                    stop=False,
+                )
+
+        def mix(c, j0, width, taken, on_scalar=True):
             blocks = width // P
             a = j0 // HALF
             nc.vector.tensor_tensor(
@@ -135,11 +155,9 @@ def tile_picked_treeup_gelu_p_kernel(
                 share_sb[a][:, j0 - HALF * a : j0 - HALF * a + width],
                 MULT,
             )
-            bank = psum.tile([P, blocks, P], F32, name="zt", tag="zt", bufs=3)
-            for b in range(blocks):
-                nc.tensor.matmul(
-                    bank[:, b, :], lhsT=h[c][:, j0 + P * b : j0 + P * (b + 1)], rhs=ident[:], is_transpose=True, start=(b == 0), stop=False
-                )
+            if (c, j0) not in sums:
+                begin(c, j0, width, "zt")
+            bank = sums[c, j0]
             for b in range(blocks):
                 nc.tensor.matmul(
                     bank[:, b, :], lhsT=taken[:, P * b : P * (b + 1)], rhs=ident[:], is_transpose=True, start=False, stop=(b == blocks - 1)
@@ -147,21 +165,23 @@ def tile_picked_treeup_gelu_p_kernel(
             for q, (j, w) in enumerate(STRETCHES):
                 if j0 <= j < j0 + width:
                     b0 = (j - j0) // P
-                    nc.scalar.copy(
-                        z_rows[q][:, :, :, 32 * c : 32 * (c + 1), :],
-                        bank[:, b0 : b0 + w // P, :].rearrange("j b (p u e) -> j b u p e", u=2, e=2),
-                    )
+                    dst = z_rows[q][:, :, :, 32 * c : 32 * (c + 1), :]
+                    src = bank[:, b0 : b0 + w // P, :].rearrange("j b (p u e) -> j b u p e", u=2, e=2)
+                    if on_scalar:
+                        nc.scalar.copy(dst, src)
+                    else:
+                        nc.vector.tensor_copy(dst, src)
 
         z_bf = {}
         acc = {}
 
-        def turn(q, on_scalar, slot):
+        def turn(q, on_scalar, slot, ring):
             j, w = PIECES[q]
             s = [k for k, (j1, w1s) in enumerate(STRETCHES) if j1 <= j < j1 + w1s][0]
             b0 = (j - STRETCHES[s][0]) // P
             words = z_rows[s][:].rearrange("j b u p e -> j (b u p e)").bitcast(F32)
             blocks = w // P
-            bank = psum.tile([P, blocks, 2, P], F32, name="zw", tag="zw", bufs=2)
+            bank = psum.tile([P, blocks, 2, P], F32, name="zw", tag=ring, bufs=RINGS[ring])
             for b in range(blocks):
                 for u in range(2):
                     m0 = P * (2 * (b0 + b) + u)
@@ -174,12 +194,12 @@ def tile_picked_treeup_gelu_p_kernel(
             else:
                 nc.vector.tensor_copy(dst, src)
 
-        def second_layer(q):
+        def second_layer(q, ring):
             w = PIECES[q][1]
             z_codes = keep.tile([P, w], U32, name="z_codes%d" % q, align_bytes=64)
             z_plane = keep.tile([P, w], U8, name="z_plane%d" % q, align_bytes=64)
             nc.vector.quantize_mx(out=z_codes[:].bitcast(FP8X4), scales=z_plane[:], in_=z_bf[q][:])
-            acc[q] = psum.tile([P, w], F32, name="acc", tag="pre", bufs=3)
+            acc[q] = psum.tile([P, w], F32, name="acc", tag=ring, bufs=RINGS[ring])
             nc.tensor.matmul_mx(
                 acc[q][:],
                 lhsT=w2_codes[:].bitcast(FP8X4),
@@ -231,19 +251,19 @@ def tile_picked_treeup_gelu_p_kernel(
         mix(3, 0, HALF, room("taken2", HALF))
         last = room("share0", S)
         mix(2, HALF, HALF, last[:, 0:HALF])
-        turn(0, True, "z0")
+        turn(0, False, "share1", "zw")
         mix(3, 512, 256, last[:, 512:768])
         mix(3, 768, 128, last[:, 768:896])
         mix(3, 896, 128, last[:, 896:1024])
-        turn(1, False, "share1")
-        second_layer(0)
-        turn(2, True, "z2")
-        second_layer(1)
-        turn(3, False, "z3")
-        turn(4, True, "z4")
-        second_layer(2)
-        second_layer(3)
-        second_layer(4)
+        turn(1, False, "z1", "zw")
+        second_layer(0, "zt")
+        second_layer(1, "zt")
+        turn(2, True, "z2", "pre")
+        turn(3, True, "z3", "pre")
+        turn(4, True, "z4", "pre")
+        second_layer(2, "zt")
+        second_layer(3, "zw")
+        second_layer(4, "zw")
         finish(0, True)
         finish(1, True)
         finish(2, False)

@@ -17,13 +17,18 @@ GELU = mybir.ActivationFunctionType.Gelu_apprx_tanh
 MULT = mybir.AluOpType.mult
 
 P = 128
-PASSES = K // 512
+PACK = 4
+PASS = P * PACK
+PASSES = K // PASS
 CHUNKS = H // P
+QUADRANTS = 4
+LIST_ROWS = 16
 HALF = S // 2
-QUARTER = S // 4
+BANKS_PER_RING = 4
+
+W1_LOADS = ((0, 1), (1, 3), (3, 4))
 STRETCHES = ((0, 512), (512, 256), (768, 128), (896, 128))
-RINGS = {"pre": 3, "zt": 3, "zw": 2}
-PIECES = ((0, 256), (256, 256), (512, 256), (768, 128), (896, 128))
+STEPS = ((0, 256), (256, 256), (512, 256), (768, 128), (896, 128))
 
 
 def tile_picked_treeup_gelu_p_kernel(
@@ -34,91 +39,123 @@ def tile_picked_treeup_gelu_p_kernel(
         keep = ctx.enter_context(tc.tile_pool(name="keep", bufs=1))
         psum = ctx.enter_context(tc.psum_pool(name="psum", bufs=1))
 
-        offs_sb = keep.tile([P, S // 16], U16, name="offs_sb")
-        par_sb = keep.tile([P, S // 16], U16, name="par_sb")
+        def bank_of(ring, shape):
+            return psum.tile(shape, F32, name="bank", tag=ring, bufs=BANKS_PER_RING)
+
+        def copy(on_scalar, dst, src):
+            if on_scalar:
+                nc.scalar.copy(dst, src)
+            else:
+                nc.vector.tensor_copy(dst, src)
+
+        offs_sb = keep.tile([P, S // LIST_ROWS], U16, name="offs_sb")
+        par_sb = keep.tile([P, S // LIST_ROWS], U16, name="par_sb")
         x_table = [keep.tile([P, T], U32, name="x_table%d" % g) for g in range(PASSES)]
-        xs_table = keep.tile([P, T], U8, name="xs_table")
-        spans = ((0, 1), (1, 3), (3, 4))
-        w1_raw = [[keep.tile([P, 4, P * (hi - lo)], F32, name="w1_raw%d_%d" % (lo, g), tag="raw%d_%d" % (lo, g)) for g in range(PASSES)] for lo, hi in spans]
-        share_sb = [keep.tile([P, HALF], F32, name="share%d" % a, tag="share%d" % a, align_bytes=64) for a in range(2)]
+        x_scale_table = keep.tile([P, T], U8, name="x_scale_table")
+        w1_raw = [
+            [keep.tile([P, PACK, P * (hi - lo)], F32, name="w1_raw", tag="w1_raw%d_%d" % (lo, g)) for g in range(PASSES)]
+            for lo, hi in W1_LOADS
+        ]
+        share_sb = [keep.tile([P, HALF], F32, name="share_sb", tag="share%d" % a, align_bytes=64) for a in range(2)]
         w2_codes = keep.tile([P, N], U32, name="w2_codes", align_bytes=64)
         w2_plane = keep.tile([P, N], U8, name="w2_plane", align_bytes=64)
         ident = keep.tile([P, P], F32, name="ident")
 
-        nc.gpsimd.memset(xs_table[:].bitcast(I32), 0)
+        nc.gpsimd.memset(x_scale_table[:].bitcast(I32), 0)
         warm_in = keep.tile([P, 1], F32, name="warm_in")
         warm_out = keep.tile([P, 1], F32, name="warm_out")
         nc.vector.memset(warm_in[:], 0.0)
         nc.scalar.activation(warm_out[:], warm_in[:], GELU)
+
         nc.sync.dma_start(offs_sb[:], offs)
         nc.sync.dma_start(par_sb[:], par)
-        for q in range(4):
-            nc.sync.dma_start(out=xs_table[32 * q : 32 * q + 8, :].bitcast(I32), in_=x_scales[:, 4 * q : 4 * q + 4, :].bitcast(I32))
+        for q in range(QUADRANTS):
+            nc.sync.dma_start(
+                out=x_scale_table[32 * q : 32 * q + 4 * PASSES, :].bitcast(I32),
+                in_=x_scales[:, 4 * q : 4 * q + 4, :].bitcast(I32),
+            )
 
         def load_x(g):
             nc.sync.dma_start(out=x_table[g][:].bitcast(I32), in_=x_words[g].rearrange("p n t -> p (n t)").bitcast(I32))
 
-        def load_w1(s, g):
-            lo, hi = spans[s]
+        def load_w1(n, g):
+            lo, hi = W1_LOADS[n]
             nc.sync.dma_start(
-                out=w1_raw[s][g][:],
-                in_=w1[512 * g : 512 * (g + 1), P * lo : P * hi].rearrange("(p r) m -> p r m", r=4),
+                out=w1_raw[n][g][:],
+                in_=w1[PASS * g : PASS * (g + 1), P * lo : P * hi].rearrange("(p r) m -> p r m", r=PACK),
             )
+
+        def load_share(a):
+            nc.sync.dma_start(out=share_sb[a][:], in_=share[:, HALF * a : HALF * (a + 1)])
 
         load_x(0)
         load_w1(0, 0)
         load_w1(0, 1)
         load_x(1)
         load_w1(1, 0)
-        nc.sync.dma_start(out=share_sb[0][:], in_=share[:, 0:HALF])
+        load_share(0)
         load_w1(1, 1)
-        nc.sync.dma_start(out=share_sb[1][:], in_=share[:, HALF:S])
         load_w1(2, 0)
         load_w1(2, 1)
+        load_share(1)
         nc.gpsimd.memset(w2_plane[:], 0)
         make_identity(nc, ident[:])
         nc.sync.dma_start(out=w2_codes[:].bitcast(I32), in_=w2_words[0].rearrange("p n t -> p (n t)").bitcast(I32))
-        for q in range(4):
-            nc.sync.dma_start(out=w2_plane[32 * q : 32 * q + 4, :].bitcast(I32), in_=w2_scales[0, 4 * q : 4 * q + 4, :].bitcast(I32))
+        for q in range(QUADRANTS):
+            nc.sync.dma_start(
+                out=w2_plane[32 * q : 32 * q + 4, :].bitcast(I32), in_=w2_scales[0, 4 * q : 4 * q + 4, :].bitcast(I32)
+            )
 
         x_plane = keep.tile([P, S], U8, name="x_plane", align_bytes=64)
-        x_codes = [{}, {}]
+        x_codes = {}
 
-        def gather_x(g, a, slot):
-            x_codes[g][a] = keep.tile([P, HALF], U32, name="x_codes", tag=slot, align_bytes=64)
-            nc.vector.tensor_copy(x_codes[g][a][:], x_table[g][:].indirect(offs_sb[:, 32 * a : 32 * (a + 1)]))
+        def list_slice(list_sb, first, count):
+            return list_sb[:, first // LIST_ROWS : (first + count) // LIST_ROWS]
 
-        w1_bf = [[keep.tile([P, P, 4], BF16, name="w1_bf%d_%d" % (c, g), tag="stage%d_%d" % (c, g), align_bytes=64) for g in range(PASSES)] for c in range(CHUNKS)]
-        w1_codes = [[keep.tile([P, P], U32, name="w1_codes%d_%d" % (c, g), align_bytes=64) for g in range(PASSES)] for c in range(CHUNKS)]
-        w1_plane = [[keep.tile([P, P], U8, name="w1_plane%d_%d" % (c, g), align_bytes=64) for g in range(PASSES)] for c in range(CHUNKS)]
+        def gather_x(g):
+            for a in range(2):
+                x_codes[g, a] = keep.tile([P, HALF], U32, name="x_codes%d_%d" % (g, a), align_bytes=64)
+                nc.vector.tensor_copy(x_codes[g, a][:], x_table[g][:].indirect(list_slice(offs_sb, HALF * a, HALF)))
 
-        def cast_w1(c, g):
-            dst = w1_bf[c][g][:].rearrange("p (m i) r -> p m r i", i=4)
-            s = [k for k in range(3) if spans[k][0] <= c < spans[k][1]][0]
-            m0 = P * (c - spans[s][0])
-            src = w1_raw[s][g][:, :, m0 : m0 + P].rearrange("p r (m i) -> p m r i", i=4)
-            if (c, g) in ((0, 0), (0, 1), (1, 0), (2, 0), (2, 1), (3, 0), (3, 1)):
-                nc.scalar.copy(dst, src)
-            else:
-                nc.vector.tensor_copy(dst, src)
+        w1_bf = [
+            [keep.tile([P, P, PACK], BF16, name="w1_bf", tag="w1_bf%d_%d" % (c, g), align_bytes=64) for g in range(PASSES)]
+            for c in range(CHUNKS)
+        ]
+        w1_codes = [
+            [keep.tile([P, P], U32, name="w1_codes%d_%d" % (c, g), align_bytes=64) for g in range(PASSES)] for c in range(CHUNKS)
+        ]
+        w1_plane = [
+            [keep.tile([P, P], U8, name="w1_plane%d_%d" % (c, g), align_bytes=64) for g in range(PASSES)] for c in range(CHUNKS)
+        ]
+
+        def cast_w1(c, g, on_scalar=True):
+            n = [k for k, (lo, hi) in enumerate(W1_LOADS) if lo <= c < hi][0]
+            m0 = P * (c - W1_LOADS[n][0])
+            copy(
+                on_scalar,
+                w1_bf[c][g][:].rearrange("p (m i) r -> p m r i", i=4),
+                w1_raw[n][g][:, :, m0 : m0 + P].rearrange("p r (m i) -> p m r i", i=4),
+            )
 
         def quantize_w1(c, g):
             nc.vector.quantize_mx(
-                out=w1_codes[c][g][:].bitcast(FP8X4), scales=w1_plane[c][g][:], in_=w1_bf[c][g][:].rearrange("p m r -> p (m r)")
+                out=w1_codes[c][g][:].bitcast(FP8X4),
+                scales=w1_plane[c][g][:],
+                in_=w1_bf[c][g][:].rearrange("p m r -> p (m r)"),
             )
 
         h = {}
 
-        def first_layer(c, slot):
-            h[c] = keep.tile([P, S], F32, name="h%d" % c, tag=slot)
-            banks = [psum.tile([P, HALF], F32, name="pre", tag="pre", bufs=3) for a in range(2)]
+        def first_layer(c, tag):
+            h[c] = keep.tile([P, S], F32, name="h", tag=tag)
+            banks = [bank_of("products", [P, HALF]) for a in range(2)]
             for g in range(PASSES):
                 for a in range(2):
                     nc.tensor.matmul_mx(
                         banks[a][:],
                         lhsT=w1_codes[c][g][:].bitcast(FP8X4),
                         lhsT_scale=w1_plane[c][g][:],
-                        rhs=x_codes[g][a][:].bitcast(FP8X4),
+                        rhs=x_codes[g, a][:].bitcast(FP8X4),
                         rhs_scale=x_plane[4 * g : P, HALF * a : HALF * (a + 1)],
                         start=(g == 0),
                         stop=(g == PASSES - 1),
@@ -126,80 +163,74 @@ def tile_picked_treeup_gelu_p_kernel(
             for a in range(2):
                 nc.scalar.activation(h[c][:, HALF * a : HALF * (a + 1)], banks[a][:], GELU)
 
-        z_rows = [keep.tile([P, w // P, 2, P, 2], BF16, name="z_rows%d" % q) for q, (j, w) in enumerate(STRETCHES)]
+        z_rows = [keep.tile([P, w // P, 2, P, 2], BF16, name="z_rows%d" % s) for s, (j, w) in enumerate(STRETCHES)]
 
-        def room(slot, width):
-            return keep.tile([P, width], F32, name="taken", tag=slot, align_bytes=64)
+        def staging(tag, width):
+            return keep.tile([P, width], F32, name="taken", tag=tag, align_bytes=64)
 
-        sums = {}
-
-        def begin(c, j0, width, ring):
+        def mix(c, j0, width, taken):
             blocks = width // P
-            sums[c, j0] = psum.tile([P, blocks, P], F32, name="zt", tag=ring, bufs=RINGS[ring])
+            a = j0 // HALF
+            nc.vector.tensor_tensor(
+                taken[:],
+                h[c][:].indirect(list_slice(par_sb, j0, width)),
+                share_sb[a][:, j0 - HALF * a : j0 - HALF * a + width],
+                MULT,
+            )
+            bank = bank_of("sums", [P, blocks, P])
             for b in range(blocks):
                 nc.tensor.matmul(
-                    sums[c, j0][:, b, :],
+                    bank[:, b, :],
                     lhsT=h[c][:, j0 + P * b : j0 + P * (b + 1)],
                     rhs=ident[:],
                     is_transpose=True,
                     start=(b == 0),
                     stop=False,
                 )
-
-        def mix(c, j0, width, taken, on_scalar=True):
-            blocks = width // P
-            a = j0 // HALF
-            nc.vector.tensor_tensor(
-                taken[:],
-                h[c][:].indirect(par_sb[:, j0 // 16 : (j0 + width) // 16]),
-                share_sb[a][:, j0 - HALF * a : j0 - HALF * a + width],
-                MULT,
-            )
-            if (c, j0) not in sums:
-                begin(c, j0, width, "zt")
-            bank = sums[c, j0]
             for b in range(blocks):
                 nc.tensor.matmul(
-                    bank[:, b, :], lhsT=taken[:, P * b : P * (b + 1)], rhs=ident[:], is_transpose=True, start=False, stop=(b == blocks - 1)
+                    bank[:, b, :],
+                    lhsT=taken[:, P * b : P * (b + 1)],
+                    rhs=ident[:],
+                    is_transpose=True,
+                    start=False,
+                    stop=(b == blocks - 1),
                 )
-            for q, (j, w) in enumerate(STRETCHES):
+            for s, (j, w) in enumerate(STRETCHES):
                 if j0 <= j < j0 + width:
                     b0 = (j - j0) // P
-                    dst = z_rows[q][:, :, :, 32 * c : 32 * (c + 1), :]
-                    src = bank[:, b0 : b0 + w // P, :].rearrange("j b (p u e) -> j b u p e", u=2, e=2)
-                    if on_scalar:
-                        nc.scalar.copy(dst, src)
-                    else:
-                        nc.vector.tensor_copy(dst, src)
+                    nc.scalar.copy(
+                        z_rows[s][:, :, :, 32 * c : 32 * (c + 1), :],
+                        bank[:, b0 : b0 + w // P, :].rearrange("j b (p u e) -> j b u p e", u=2, e=2),
+                    )
 
         z_bf = {}
         acc = {}
 
-        def turn(q, on_scalar, slot, ring):
-            j, w = PIECES[q]
-            s = [k for k, (j1, w1s) in enumerate(STRETCHES) if j1 <= j < j1 + w1s][0]
-            b0 = (j - STRETCHES[s][0]) // P
-            words = z_rows[s][:].rearrange("j b u p e -> j (b u p e)").bitcast(F32)
+        def turn_back(q, on_scalar, tag):
+            j0, w = STEPS[q]
+            s = [k for k, (j, width) in enumerate(STRETCHES) if j <= j0 < j + width][0]
+            b0 = (j0 - STRETCHES[s][0]) // P
+            pairs = z_rows[s][:].rearrange("j b u p e -> j (b u p e)").bitcast(F32)
             blocks = w // P
-            bank = psum.tile([P, blocks, 2, P], F32, name="zw", tag=ring, bufs=RINGS[ring])
+            bank = bank_of("products", [P, blocks, 2, P])
             for b in range(blocks):
                 for u in range(2):
                     m0 = P * (2 * (b0 + b) + u)
-                    nc.tensor.transpose(bank[:, b, u, :], words[:, m0 : m0 + P], ident[:])
-            z_bf[q] = keep.tile([P, 4 * w], BF16, name="z_bf", tag=slot, align_bytes=64)
-            dst = z_bf[q][:].bitcast(F32).rearrange("p (b j u) -> p b j u", b=blocks, u=2)
-            src = bank[:].rearrange("p b u j -> p b j u")
-            if on_scalar:
-                nc.scalar.copy(dst, src)
-            else:
-                nc.vector.tensor_copy(dst, src)
+                    nc.tensor.transpose(bank[:, b, u, :], pairs[:, m0 : m0 + P], ident[:])
+            z_bf[q] = keep.tile([P, PACK * w], BF16, name="z_bf", tag=tag, align_bytes=64)
+            copy(
+                on_scalar,
+                z_bf[q][:].bitcast(F32).rearrange("p (b j u) -> p b j u", b=blocks, u=2),
+                bank[:].rearrange("p b u j -> p b j u"),
+            )
 
         def second_layer(q, ring):
-            w = PIECES[q][1]
+            w = STEPS[q][1]
             z_codes = keep.tile([P, w], U32, name="z_codes%d" % q, align_bytes=64)
             z_plane = keep.tile([P, w], U8, name="z_plane%d" % q, align_bytes=64)
             nc.vector.quantize_mx(out=z_codes[:].bitcast(FP8X4), scales=z_plane[:], in_=z_bf[q][:])
-            acc[q] = psum.tile([P, w], F32, name="acc", tag=ring, bufs=RINGS[ring])
+            acc[q] = bank_of(ring, [P, w])
             nc.tensor.matmul_mx(
                 acc[q][:],
                 lhsT=w2_codes[:].bitcast(FP8X4),
@@ -210,62 +241,55 @@ def tile_picked_treeup_gelu_p_kernel(
                 stop=True,
             )
 
-        def finish(q, on_scalar):
-            j, w = PIECES[q]
-            res = keep.tile([P, w], F32, name="res%d" % q)
-            if on_scalar:
-                nc.scalar.copy(res[:], acc[q][:])
-            else:
-                nc.vector.tensor_copy(res[:], acc[q][:])
-            nc.sync.dma_start(out=out[:, j : j + w], in_=res[:])
+        def store(q, on_scalar):
+            j0, w = STEPS[q]
+            result = keep.tile([P, w], F32, name="result%d" % q)
+            copy(on_scalar, result[:], acc[q][:])
+            nc.sync.dma_start(out=out[:, j0 : j0 + w], in_=result[:])
 
-        nc.vector.tensor_copy(x_plane[:], xs_table[:].indirect(offs_sb[:]))
-        gather_x(0, 0, "x00")
-        gather_x(0, 1, "x01")
+        nc.vector.tensor_copy(x_plane[:], x_scale_table[:].indirect(offs_sb[:]))
+        gather_x(0)
         for g in range(PASSES):
             cast_w1(0, g)
             quantize_w1(0, g)
-        gather_x(1, 0, "x10")
-        gather_x(1, 1, "x11")
+        gather_x(1)
+
         cast_w1(1, 0)
         cast_w1(2, 0)
-        first_layer(0, "raw1_0")
+        first_layer(0, "w1_raw1_0")
         quantize_w1(1, 0)
-        cast_w1(1, 1)
+        cast_w1(1, 1, on_scalar=False)
         quantize_w1(2, 0)
         quantize_w1(1, 1)
         cast_w1(2, 1)
-        first_layer(1, "h1")
         for g in range(PASSES):
             cast_w1(3, g)
-        mix(0, 0, HALF, room("stage1_1", HALF))
+        first_layer(1, "h1")
+
+        mix(0, 0, HALF, staging("w1_bf1_1", HALF))
         quantize_w1(2, 1)
         first_layer(2, "h2")
-        mix(0, HALF, HALF, room("stage2_1", HALF))
-        mix(1, 0, HALF, room("taken0", HALF))
+        mix(0, HALF, HALF, staging("taken0", HALF))
         for g in range(PASSES):
             quantize_w1(3, g)
         first_layer(3, "h3")
-        mix(1, HALF, HALF, room("stage3_1", HALF))
-        mix(2, 0, HALF, room("taken1", HALF))
-        mix(3, 0, HALF, room("taken2", HALF))
-        last = room("share0", S)
-        mix(2, HALF, HALF, last[:, 0:HALF])
-        turn(0, False, "share1", "zw")
-        mix(3, 512, 256, last[:, 512:768])
-        mix(3, 768, 128, last[:, 768:896])
-        mix(3, 896, 128, last[:, 896:1024])
-        turn(1, False, "z1", "zw")
-        second_layer(0, "zt")
-        second_layer(1, "zt")
-        turn(2, True, "z2", "pre")
-        turn(3, True, "z3", "pre")
-        turn(4, True, "z4", "pre")
-        second_layer(2, "zt")
-        second_layer(3, "zw")
-        second_layer(4, "zw")
-        finish(0, True)
-        finish(1, True)
-        finish(2, False)
-        finish(3, True)
-        finish(4, False)
+        mix(1, 0, HALF, staging("taken1", HALF))
+        mix(1, HALF, HALF, staging("taken2", HALF))
+
+        mix(2, 0, HALF, staging("taken3", HALF))
+        mix(3, 0, HALF, staging("taken4", HALF))
+        late = staging("share0", S)
+        mix(2, HALF, HALF, late[:, 0:HALF])
+        turn_back(0, False, "share1")
+        for j0, w in STRETCHES[1:]:
+            mix(CHUNKS - 1, j0, w, late[:, j0 : j0 + w])
+        turn_back(1, False, "z_bf1")
+        second_layer(0, "sums")
+        second_layer(1, "sums")
+        for q in range(2, len(STEPS)):
+            turn_back(q, True, "z_bf%d" % q)
+        second_layer(2, "sums")
+        second_layer(3, "sums")
+        second_layer(4, "products")
+        for q in range(len(STEPS)):
+            store(q, on_scalar=(q < 2 or q % 2 == 1))

@@ -57,6 +57,7 @@ def tile_picked_treeup_gelu_p_kernel(
             for lo, hi in W1_LOADS
         ]
         share_sb = [keep.tile([P, HALF], F32, name="share_sb", tag="share%d" % a, align_bytes=64) for a in range(2)]
+        share_cols = keep.tile([P, 2, HALF // P], F32, name="share_cols")
         w2_codes = keep.tile([P, N], U32, name="w2_codes", align_bytes=64)
         w2_plane = keep.tile([P, N], U8, name="w2_plane", align_bytes=64)
         ident = keep.tile([P, P], F32, name="ident")
@@ -68,42 +69,39 @@ def tile_picked_treeup_gelu_p_kernel(
         nc.scalar.activation(warm_out[:], warm_in[:], GELU)
 
         nc.sync.dma_start(offs_sb[:], offs)
-        nc.sync.dma_start(par_sb[:], par)
-        for q in range(QUADRANTS):
+        nc.sync.dma_start(out=share_cols[:], in_=share[0].rearrange("(a p b) -> p a b", a=2, b=HALF // P))
+        for quad in range(QUADRANTS):
             nc.sync.dma_start(
-                out=x_scale_table[32 * q : 32 * q + 4 * PASSES, :].bitcast(I32),
-                in_=x_scales[:, 4 * q : 4 * q + 4, :].bitcast(I32),
+                out=x_scale_table[32 * quad : 32 * quad + 4 * PASSES, :].bitcast(I32),
+                in_=x_scales[:, 4 * quad : 4 * quad + 4, :].bitcast(I32),
             )
 
         def load_x(g):
             nc.sync.dma_start(out=x_table[g][:].bitcast(I32), in_=x_words[g].rearrange("p n t -> p (n t)").bitcast(I32))
 
-        def load_w1(n, g):
-            lo, hi = W1_LOADS[n]
+        def load_w1(load, g):
+            lo, hi = W1_LOADS[load]
             nc.sync.dma_start(
-                out=w1_raw[n][g][:],
+                out=w1_raw[load][g][:],
                 in_=w1[PASS * g : PASS * (g + 1), P * lo : P * hi].rearrange("(p r) m -> p r m", r=PACK),
             )
-
-        def load_share(a):
-            nc.sync.dma_start(out=share_sb[a][:], in_=share[:, HALF * a : HALF * (a + 1)])
 
         load_x(0)
         load_w1(0, 0)
         load_w1(0, 1)
         load_x(1)
         load_w1(1, 0)
-        load_share(0)
+        nc.sync.dma_start(par_sb[:], par)
         load_w1(1, 1)
         load_w1(2, 0)
         load_w1(2, 1)
-        load_share(1)
         nc.gpsimd.memset(w2_plane[:], 0)
         make_identity(nc, ident[:])
         nc.sync.dma_start(out=w2_codes[:].bitcast(I32), in_=w2_words[0].rearrange("p n t -> p (n t)").bitcast(I32))
-        for q in range(QUADRANTS):
+        for quad in range(QUADRANTS):
             nc.sync.dma_start(
-                out=w2_plane[32 * q : 32 * q + 4, :].bitcast(I32), in_=w2_scales[0, 4 * q : 4 * q + 4, :].bitcast(I32)
+                out=w2_plane[32 * quad : 32 * quad + 4, :].bitcast(I32),
+                in_=w2_scales[0, 4 * quad : 4 * quad + 4, :].bitcast(I32),
             )
 
         x_plane = keep.tile([P, S], U8, name="x_plane", align_bytes=64)
@@ -129,12 +127,12 @@ def tile_picked_treeup_gelu_p_kernel(
         ]
 
         def cast_w1(c, g, on_scalar=True):
-            n = [k for k, (lo, hi) in enumerate(W1_LOADS) if lo <= c < hi][0]
-            m0 = P * (c - W1_LOADS[n][0])
+            load = [number for number, (lo, hi) in enumerate(W1_LOADS) if lo <= c < hi][0]
+            m0 = P * (c - W1_LOADS[load][0])
             copy(
                 on_scalar,
-                w1_bf[c][g][:].rearrange("p (m i) r -> p m r i", i=4),
-                w1_raw[n][g][:, :, m0 : m0 + P].rearrange("p r (m i) -> p m r i", i=4),
+                w1_bf[c][g][:].rearrange("p (m n) r -> p m r n", n=4),
+                w1_raw[load][g][:, :, m0 : m0 + P].rearrange("p r (m n) -> p m r n", n=4),
             )
 
         def quantize_w1(c, g):
@@ -209,15 +207,15 @@ def tile_picked_treeup_gelu_p_kernel(
 
         def turn_back(q, on_scalar, tag):
             j0, w = STEPS[q]
-            s = [k for k, (j, width) in enumerate(STRETCHES) if j <= j0 < j + width][0]
+            s = [number for number, (j, width) in enumerate(STRETCHES) if j <= j0 < j + width][0]
             b0 = (j0 - STRETCHES[s][0]) // P
             pairs = z_rows[s][:].rearrange("j b u p e -> j (b u p e)").bitcast(F32)
             blocks = w // P
             bank = bank_of("products", [P, blocks, 2, P])
             for b in range(blocks):
                 for u in range(2):
-                    m0 = P * (2 * (b0 + b) + u)
-                    nc.tensor.transpose(bank[:, b, u, :], pairs[:, m0 : m0 + P], ident[:])
+                    word0 = P * (2 * (b0 + b) + u)
+                    nc.tensor.transpose(bank[:, b, u, :], pairs[:, word0 : word0 + P], ident[:])
             z_bf[q] = keep.tile([P, PACK * w], BF16, name="z_bf", tag=tag, align_bytes=64)
             copy(
                 on_scalar,
@@ -252,6 +250,11 @@ def tile_picked_treeup_gelu_p_kernel(
         for g in range(PASSES):
             cast_w1(0, g)
             quantize_w1(0, g)
+        for a in range(2):
+            bank = bank_of("sums", [P, HALF // P, P])
+            for b in range(HALF // P):
+                nc.tensor.transpose(bank[:, b, :], share_cols[:, a, b : b + 1].to_broadcast([P, P]), ident[:])
+            nc.scalar.copy(share_sb[a][:].rearrange("m (n b) -> m n b", b=HALF // P), bank[:].rearrange("m b n -> m n b"))
         gather_x(1)
 
         cast_w1(1, 0)
@@ -269,15 +272,15 @@ def tile_picked_treeup_gelu_p_kernel(
         mix(0, 0, HALF, staging("w1_bf1_1", HALF))
         quantize_w1(2, 1)
         first_layer(2, "h2")
-        mix(0, HALF, HALF, staging("taken0", HALF))
+        mix(0, HALF, HALF, staging("w1_bf2_1", HALF))
         for g in range(PASSES):
             quantize_w1(3, g)
         first_layer(3, "h3")
-        mix(1, 0, HALF, staging("taken1", HALF))
-        mix(1, HALF, HALF, staging("taken2", HALF))
+        mix(1, 0, HALF, staging("taken0", HALF))
+        mix(1, HALF, HALF, staging("taken1", HALF))
 
-        mix(2, 0, HALF, staging("taken3", HALF))
-        mix(3, 0, HALF, staging("taken4", HALF))
+        mix(2, 0, HALF, staging("taken2", HALF))
+        mix(3, 0, HALF, staging("taken3", HALF))
         late = staging("share0", S)
         mix(2, HALF, HALF, late[:, 0:HALF])
         turn_back(0, False, "share1")

@@ -24,11 +24,10 @@ CHUNKS = H // P
 QUADRANTS = 4
 LIST_ROWS = 16
 HALF = S // 2
-BANKS_PER_RING = 4
 
-W1_LOADS = ((0, 1), (1, 3), (3, 4))
-STRETCHES = ((0, 512), (512, 256), (768, 128), (896, 128))
-STEPS = ((0, 256), (256, 256), (512, 256), (768, 128), (896, 128))
+W1_LOADS = ((0, 1), (1, 2), (2, 4))
+STEPS = ((0, 512), (512, 256), (768, 128), (896, 128))
+PAIR_NODES = 256
 
 
 def tile_picked_treeup_gelu_p_kernel(
@@ -39,8 +38,11 @@ def tile_picked_treeup_gelu_p_kernel(
         keep = ctx.enter_context(tc.tile_pool(name="keep", bufs=1))
         psum = ctx.enter_context(tc.psum_pool(name="psum", bufs=1))
 
-        def bank_of(ring, shape):
-            return psum.tile(shape, F32, name="bank", tag=ring, bufs=BANKS_PER_RING)
+        def bank_tile(number, shape):
+            return psum.tile(shape, F32, name="bank", tag="bank%d" % number)
+
+        def sbuf(tag, shape, dtype):
+            return keep.tile(shape, dtype, name=tag, tag=tag, align_bytes=64)
 
         def copy(on_scalar, dst, src):
             if on_scalar:
@@ -50,34 +52,24 @@ def tile_picked_treeup_gelu_p_kernel(
 
         offs_sb = keep.tile([P, S // LIST_ROWS], U16, name="offs_sb")
         par_sb = keep.tile([P, S // LIST_ROWS], U16, name="par_sb")
-        x_table = [keep.tile([P, T], U32, name="x_table%d" % g) for g in range(PASSES)]
-        x_scale_table = keep.tile([P, T], U8, name="x_scale_table")
-        w1_raw = [
-            [keep.tile([P, PACK, P * (hi - lo)], F32, name="w1_raw", tag="w1_raw%d_%d" % (lo, g)) for g in range(PASSES)]
-            for lo, hi in W1_LOADS
-        ]
-        share_sb = [keep.tile([P, HALF], F32, name="share_sb", tag="share%d" % a, align_bytes=64) for a in range(2)]
-        share_cols = keep.tile([P, 2, HALF // P], F32, name="share_cols")
-        w2_codes = keep.tile([P, N], U32, name="w2_codes", align_bytes=64)
-        w2_plane = keep.tile([P, N], U8, name="w2_plane", align_bytes=64)
-        ident = keep.tile([P, P], F32, name="ident")
+        x_table = [sbuf("x_table%d" % g, [P, T], U32) for g in range(PASSES)]
+        x_scale_table = sbuf("x_scale_table", [P, T], U8)
+        w1_raw = [[sbuf("w1_raw%d_%d" % (lo, g), [P, PACK, P * (hi - lo)], F32) for g in range(PASSES)] for lo, hi in W1_LOADS]
+        share_sb = [sbuf("share%d" % a, [P, HALF], F32) for a in range(2)]
+        share_cols = sbuf("share_cols", [P, 2, HALF // P], F32)
+        w2_codes = sbuf("w2_codes", [P, N], U32)
+        w2_plane = sbuf("w2_plane", [P, N], U8)
+        ident = sbuf("ident", [P, P], F32)
 
         nc.gpsimd.memset(x_scale_table[:].bitcast(I32), 0)
-        warm_in = keep.tile([P, 1], F32, name="warm_in")
-        warm_out = keep.tile([P, 1], F32, name="warm_out")
+        warm_in = sbuf("warm_in", [P, 1], F32)
+        warm_out = sbuf("warm_out", [P, 1], F32)
         nc.vector.memset(warm_in[:], 0.0)
         nc.scalar.activation(warm_out[:], warm_in[:], GELU)
 
-        nc.sync.dma_start(offs_sb[:], offs)
-        nc.sync.dma_start(out=share_cols[:], in_=share[0].rearrange("(a p b) -> p a b", a=2, b=HALF // P))
-        for quad in range(QUADRANTS):
-            nc.sync.dma_start(
-                out=x_scale_table[32 * quad : 32 * quad + 4 * PASSES, :].bitcast(I32),
-                in_=x_scales[:, 4 * quad : 4 * quad + 4, :].bitcast(I32),
-            )
-
-        def load_x(g):
-            nc.sync.dma_start(out=x_table[g][:].bitcast(I32), in_=x_words[g].rearrange("p n t -> p (n t)").bitcast(I32))
+        def load_x(g, lo, hi):
+            words = x_words[g].rearrange("p n t -> p (n t)").bitcast(I32)
+            nc.sync.dma_start(out=x_table[g][:, lo:hi].bitcast(I32), in_=words[:, lo:hi])
 
         def load_w1(load, g):
             lo, hi = W1_LOADS[load]
@@ -86,17 +78,24 @@ def tile_picked_treeup_gelu_p_kernel(
                 in_=w1[PASS * g : PASS * (g + 1), P * lo : P * hi].rearrange("(p r) m -> p r m", r=PACK),
             )
 
-        load_x(0)
+        nc.sync.dma_start(offs_sb[:], offs)
+        nc.sync.dma_start(out=share_cols[:], in_=share[0].rearrange("(a p b) -> p a b", a=2, b=HALF // P))
+        load_x(0, 0, T // 4)
+        for quad in range(QUADRANTS):
+            nc.sync.dma_start(
+                out=x_scale_table[32 * quad : 32 * quad + 4 * PASSES, :].bitcast(I32),
+                in_=x_scales[:, 4 * quad : 4 * quad + 4, :].bitcast(I32),
+            )
+        load_x(0, T // 4, T)
         load_w1(0, 0)
         load_w1(0, 1)
-        load_x(1)
-        load_w1(1, 0)
+        load_x(1, 0, T)
         nc.sync.dma_start(par_sb[:], par)
-        load_w1(1, 1)
-        load_w1(2, 0)
-        load_w1(2, 1)
-        nc.gpsimd.memset(w2_plane[:], 0)
+        for load in range(1, len(W1_LOADS)):
+            for g in range(PASSES):
+                load_w1(load, g)
         make_identity(nc, ident[:])
+        nc.gpsimd.memset(w2_plane[:], 0)
         nc.sync.dma_start(out=w2_codes[:].bitcast(I32), in_=w2_words[0].rearrange("p n t -> p (n t)").bitcast(I32))
         for quad in range(QUADRANTS):
             nc.sync.dma_start(
@@ -104,29 +103,17 @@ def tile_picked_treeup_gelu_p_kernel(
                 in_=w2_scales[0, 4 * quad : 4 * quad + 4, :].bitcast(I32),
             )
 
-        x_plane = keep.tile([P, S], U8, name="x_plane", align_bytes=64)
-        x_codes = {}
-
         def list_slice(list_sb, first, count):
             return list_sb[:, first // LIST_ROWS : (first + count) // LIST_ROWS]
 
-        def gather_x(g):
-            for a in range(2):
-                x_codes[g, a] = keep.tile([P, HALF], U32, name="x_codes%d_%d" % (g, a), align_bytes=64)
-                nc.vector.tensor_copy(x_codes[g, a][:], x_table[g][:].indirect(list_slice(offs_sb, HALF * a, HALF)))
+        def gather_x(dst, g, j0, width):
+            nc.vector.tensor_copy(dst, x_table[g][:].indirect(list_slice(offs_sb, j0, width)))
 
-        w1_bf = [
-            [keep.tile([P, P, PACK], BF16, name="w1_bf", tag="w1_bf%d_%d" % (c, g), align_bytes=64) for g in range(PASSES)]
-            for c in range(CHUNKS)
-        ]
-        w1_codes = [
-            [keep.tile([P, P], U32, name="w1_codes%d_%d" % (c, g), align_bytes=64) for g in range(PASSES)] for c in range(CHUNKS)
-        ]
-        w1_plane = [
-            [keep.tile([P, P], U8, name="w1_plane%d_%d" % (c, g), align_bytes=64) for g in range(PASSES)] for c in range(CHUNKS)
-        ]
+        w1_bf = [[sbuf("w1_bf%d_%d" % (c, g), [P, P, PACK], BF16) for g in range(PASSES)] for c in range(CHUNKS)]
+        w1_codes = [[sbuf("w1_codes%d_%d" % (c, g), [P, P], U32) for g in range(PASSES)] for c in range(CHUNKS)]
+        w1_plane = [[sbuf("w1_plane%d_%d" % (c, g), [P, P], U8) for g in range(PASSES)] for c in range(CHUNKS)]
 
-        def cast_w1(c, g, on_scalar=True):
+        def cast_w1(c, g, on_scalar):
             load = [number for number, (lo, hi) in enumerate(W1_LOADS) if lo <= c < hi][0]
             m0 = P * (c - W1_LOADS[load][0])
             copy(
@@ -142,157 +129,223 @@ def tile_picked_treeup_gelu_p_kernel(
                 in_=w1_bf[c][g][:].rearrange("p m r -> p (m r)"),
             )
 
+        x_codes = {}
         h = {}
+        u_banks = {}
 
-        def first_layer(c, tag):
-            h[c] = keep.tile([P, S], F32, name="h", tag=tag)
-            banks = [bank_of("products", [P, HALF]) for a in range(2)]
-            for g in range(PASSES):
-                for a in range(2):
-                    nc.tensor.matmul_mx(
-                        banks[a][:],
-                        lhsT=w1_codes[c][g][:].bitcast(FP8X4),
-                        lhsT_scale=w1_plane[c][g][:],
-                        rhs=x_codes[g, a][:].bitcast(FP8X4),
-                        rhs_scale=x_plane[4 * g : P, HALF * a : HALF * (a + 1)],
-                        start=(g == 0),
-                        stop=(g == PASSES - 1),
-                    )
-            for a in range(2):
-                nc.scalar.activation(h[c][:, HALF * a : HALF * (a + 1)], banks[a][:], GELU)
+        def open_products(c, pieces):
+            u_banks[c] = [(j0, w, bank_tile(number, [P, w])) for j0, w, number in pieces]
 
-        z_rows = [keep.tile([P, w // P, 2, P, 2], BF16, name="z_rows%d" % s) for s, (j, w) in enumerate(STRETCHES)]
+        def product_pass(c, g):
+            for j0, w, bank in u_banks[c]:
+                a = j0 // HALF
+                nc.tensor.matmul_mx(
+                    bank[:],
+                    lhsT=w1_codes[c][g][:].bitcast(FP8X4),
+                    lhsT_scale=w1_plane[c][g][:],
+                    rhs=x_codes[g, a][:, j0 - HALF * a : j0 - HALF * a + w].bitcast(FP8X4),
+                    rhs_scale=x_plane[4 * g : P, j0 : j0 + w],
+                    start=(g == 0),
+                    stop=(g == PASSES - 1),
+                )
 
-        def staging(tag, width):
-            return keep.tile([P, width], F32, name="taken", tag=tag, align_bytes=64)
+        def gelu(c, piece):
+            j0, w, bank = u_banks[c][piece]
+            nc.scalar.activation(h[c][:, j0 : j0 + w], bank[:], GELU)
 
-        def mix(c, j0, width, taken):
-            blocks = width // P
+        z_rows = sbuf("z_rows", [P, PACK * S], BF16)
+        sums = {}
+
+        def turn(bank, block, src, start, stop):
+            nc.tensor.matmul(bank[:, block, :], lhsT=src, rhs=ident[:], is_transpose=True, start=start, stop=stop)
+
+        def open_sum(name, members, number):
+            blocks = [(c, j) for c, j0, w in members for j in range(j0, j0 + w, P)]
+            bank = bank_tile(number, [P, len(blocks), P])
+            sums[name] = (members, blocks, bank)
+            for b, (c, j) in enumerate(blocks):
+                turn(bank, b, h[c][:, j : j + P], b == 0, False)
+
+        def gather_h(name, member, taken):
+            c, j0, w = sums[name][0][member]
             a = j0 // HALF
             nc.vector.tensor_tensor(
-                taken[:],
-                h[c][:].indirect(list_slice(par_sb, j0, width)),
-                share_sb[a][:, j0 - HALF * a : j0 - HALF * a + width],
+                taken,
+                h[c][:].indirect(list_slice(par_sb, j0, w)),
+                share_sb[a][:, j0 - HALF * a : j0 - HALF * a + w],
                 MULT,
             )
-            bank = bank_of("sums", [P, blocks, P])
-            for b in range(blocks):
-                nc.tensor.matmul(
-                    bank[:, b, :],
-                    lhsT=h[c][:, j0 + P * b : j0 + P * (b + 1)],
-                    rhs=ident[:],
-                    is_transpose=True,
-                    start=(b == 0),
-                    stop=False,
+
+        def add_taken(name, member, taken):
+            members, blocks, bank = sums[name]
+            c, j0, w = members[member]
+            for j in range(j0, j0 + w, P):
+                b = blocks.index((c, j))
+                turn(bank, b, taken[:, j - j0 : j - j0 + P], False, b == len(blocks) - 1)
+
+        def take(name, member, taken):
+            gather_h(name, member, taken)
+            add_taken(name, member, taken)
+
+        def round_z(name):
+            members, blocks, bank = sums[name]
+            rows = z_rows[:].rearrange("j (b u p e) -> j b u p e", u=2, p=P, e=2)
+            for c, j0, width in members:
+                b0 = blocks.index((c, j0))
+                nc.scalar.copy(
+                    rows[:, j0 // P : (j0 + width) // P, :, 32 * c : 32 * (c + 1), :],
+                    bank[:, b0 : b0 + width // P, :].rearrange("j b (p u e) -> j b u p e", u=2, e=2),
                 )
-            for b in range(blocks):
-                nc.tensor.matmul(
-                    bank[:, b, :],
-                    lhsT=taken[:, P * b : P * (b + 1)],
-                    rhs=ident[:],
-                    is_transpose=True,
-                    start=False,
-                    stop=(b == blocks - 1),
-                )
-            for s, (j, w) in enumerate(STRETCHES):
-                if j0 <= j < j0 + width:
-                    b0 = (j - j0) // P
-                    nc.scalar.copy(
-                        z_rows[s][:, :, :, 32 * c : 32 * (c + 1), :],
-                        bank[:, b0 : b0 + w // P, :].rearrange("j b (p u e) -> j b u p e", u=2, e=2),
-                    )
 
         z_bf = {}
         acc = {}
 
-        def turn_back(q, on_scalar, tag):
-            j0, w = STEPS[q]
-            s = [number for number, (j, width) in enumerate(STRETCHES) if j <= j0 < j + width][0]
-            b0 = (j0 - STRETCHES[s][0]) // P
-            pairs = z_rows[s][:].rearrange("j b u p e -> j (b u p e)").bitcast(F32)
+        def turn_back(j0, w, number, on_scalar):
+            pairs = z_rows[:].bitcast(F32)
             blocks = w // P
-            bank = bank_of("products", [P, blocks, 2, P])
+            bank = bank_tile(number, [P, blocks, 2, P])
             for b in range(blocks):
                 for u in range(2):
-                    word0 = P * (2 * (b0 + b) + u)
+                    word0 = 2 * (j0 + P * b) + P * u
                     nc.tensor.transpose(bank[:, b, u, :], pairs[:, word0 : word0 + P], ident[:])
-            z_bf[q] = keep.tile([P, PACK * w], BF16, name="z_bf", tag=tag, align_bytes=64)
+            z_bf[j0] = sbuf("z_bf%d" % j0, [P, PACK * w], BF16)
             copy(
                 on_scalar,
-                z_bf[q][:].bitcast(F32).rearrange("p (b j u) -> p b j u", b=blocks, u=2),
+                z_bf[j0][:].bitcast(F32).rearrange("p (b j u) -> p b j u", b=blocks, u=2),
                 bank[:].rearrange("p b u j -> p b j u"),
             )
 
-        def second_layer(q, ring):
-            w = STEPS[q][1]
-            z_codes = keep.tile([P, w], U32, name="z_codes%d" % q, align_bytes=64)
-            z_plane = keep.tile([P, w], U8, name="z_plane%d" % q, align_bytes=64)
-            nc.vector.quantize_mx(out=z_codes[:].bitcast(FP8X4), scales=z_plane[:], in_=z_bf[q][:])
-            acc[q] = bank_of(ring, [P, w])
+        z_codes = sbuf("z_codes", [P, S], U32)
+        z_plane = sbuf("z_plane", [P, S], U8)
+
+        def quantize_z(j0, w):
+            nc.vector.quantize_mx(
+                out=z_codes[:, j0 : j0 + w].bitcast(FP8X4), scales=z_plane[:, j0 : j0 + w], in_=z_bf[j0][:]
+            )
+
+        def second_layer(s, number):
+            j0, w = STEPS[s]
+            acc[s] = bank_tile(number, [P, w])
             nc.tensor.matmul_mx(
-                acc[q][:],
+                acc[s][:],
                 lhsT=w2_codes[:].bitcast(FP8X4),
                 lhsT_scale=w2_plane[:],
-                rhs=z_codes[:].bitcast(FP8X4),
-                rhs_scale=z_plane[:],
+                rhs=z_codes[:, j0 : j0 + w].bitcast(FP8X4),
+                rhs_scale=z_plane[:, j0 : j0 + w],
                 start=True,
                 stop=True,
             )
 
-        def store(q, on_scalar):
-            j0, w = STEPS[q]
-            result = keep.tile([P, w], F32, name="result%d" % q)
-            copy(on_scalar, result[:], acc[q][:])
+        def store(s, on_scalar, tag):
+            j0, w = STEPS[s]
+            result = sbuf(tag, [P, w], F32)
+            copy(on_scalar, result[:], acc[s][:])
             nc.sync.dma_start(out=out[:, j0 : j0 + w], in_=result[:])
 
+        x_plane = sbuf("x_plane", [P, S], U8)
         nc.vector.tensor_copy(x_plane[:], x_scale_table[:].indirect(offs_sb[:]))
-        gather_x(0)
+        for a in range(2):
+            x_codes[0, a] = sbuf("x_codes0_%d" % a, [P, HALF], U32)
+            gather_x(x_codes[0, a][:], 0, HALF * a, HALF)
         for g in range(PASSES):
-            cast_w1(0, g)
+            cast_w1(0, g, True)
             quantize_w1(0, g)
         for a in range(2):
-            bank = bank_of("sums", [P, HALF // P, P])
+            bank = bank_tile(6 + a, [P, HALF // P, P])
             for b in range(HALF // P):
                 nc.tensor.transpose(bank[:, b, :], share_cols[:, a, b : b + 1].to_broadcast([P, P]), ident[:])
             nc.scalar.copy(share_sb[a][:].rearrange("m (n b) -> m n b", b=HALF // P), bank[:].rearrange("m b n -> m n b"))
-        gather_x(1)
-
-        cast_w1(1, 0)
-        cast_w1(2, 0)
-        first_layer(0, "w1_raw1_0")
-        quantize_w1(1, 0)
-        cast_w1(1, 1, on_scalar=False)
-        quantize_w1(2, 0)
-        quantize_w1(1, 1)
-        cast_w1(2, 1)
+        x_codes[1, 0] = sbuf("x_codes1_0", [P, HALF], U32)
+        gather_x(x_codes[1, 0][:], 1, 0, HALF)
+        x_codes[1, 1] = sbuf("x_codes1_1", [P, HALF], U32)
+        for part in range(2):
+            gather_x(x_codes[1, 1][:, 256 * part : 256 * (part + 1)], 1, HALF + 256 * part, 256)
+        cast_w1(1, 0, True)
+        open_products(0, ((0, 512, 0), (512, 256, 1), (768, 256, 7)))
         for g in range(PASSES):
-            cast_w1(3, g)
-        first_layer(1, "h1")
-
-        mix(0, 0, HALF, staging("w1_bf1_1", HALF))
-        quantize_w1(2, 1)
-        first_layer(2, "h2")
-        mix(0, HALF, HALF, staging("w1_bf2_1", HALF))
+            product_pass(0, g)
+        h[0] = sbuf("w1_raw1_0", [P, S], F32)
+        for piece in range(3):
+            gelu(0, piece)
+        cast_w1(1, 1, False)
         for g in range(PASSES):
-            quantize_w1(3, g)
-        first_layer(3, "h3")
-        mix(1, 0, HALF, staging("taken0", HALF))
-        mix(1, HALF, HALF, staging("taken1", HALF))
-
-        mix(2, 0, HALF, staging("taken2", HALF))
-        mix(3, 0, HALF, staging("taken3", HALF))
-        late = staging("share0", S)
-        mix(2, HALF, HALF, late[:, 0:HALF])
-        turn_back(0, False, "share1")
-        for j0, w in STRETCHES[1:]:
-            mix(CHUNKS - 1, j0, w, late[:, j0 : j0 + w])
-        turn_back(1, False, "z_bf1")
-        second_layer(0, "sums")
-        second_layer(1, "sums")
-        for q in range(2, len(STEPS)):
-            turn_back(q, True, "z_bf%d" % q)
-        second_layer(2, "sums")
-        second_layer(3, "sums")
-        second_layer(4, "products")
-        for q in range(len(STEPS)):
-            store(q, on_scalar=(q < 2 or q % 2 == 1))
+            quantize_w1(1, g)
+        open_products(1, ((0, HALF, 2), (HALF, HALF, 3)))
+        for g in range(PASSES):
+            product_pass(1, g)
+        for c in (2, 3):
+            cast_w1(c, 0, True)
+        open_sum("00", ((0, 0, HALF),), 0)
+        open_sum("01", ((0, HALF, HALF),), 1)
+        take("00", 0, sbuf("taken00", [P, HALF], F32)[:])
+        for c in (2, 3):
+            quantize_w1(c, 0)
+            open_products(c, ((0, HALF, 2 * c), (HALF, HALF, 2 * c + 1)))
+            product_pass(c, 0)
+        taken01 = sbuf("w1_raw2_0", [P, HALF], F32)
+        gather_h("01", 0, taken01[:])
+        for c in range(1, CHUNKS):
+            h[c] = sbuf("h%d" % c, [P, S], F32)
+        gelu(1, 0)
+        cast_w1(3, 1, True)
+        gelu(1, 1)
+        cast_w1(2, 1, False)
+        for c in (2, 3):
+            quantize_w1(c, 1)
+            product_pass(c, 1)
+        add_taken("01", 0, taken01[:])
+        for c in (2, 3):
+            for piece in range(2):
+                gelu(c, piece)
+        round_z("00")
+        round_z("01")
+        open_sum("10", ((1, 0, HALF),), 2)
+        take("10", 0, sbuf("taken10", [P, HALF], F32)[:])
+        open_sum("12", ((1, 512, 256),), 3)
+        take("12", 0, sbuf("taken12", [P, 256], F32)[:])
+        open_sum("20", ((2, 0, HALF),), 4)
+        round_z("10")
+        round_z("12")
+        take("20", 0, sbuf("taken20", [P, HALF], F32)[:])
+        open_sum("30", ((3, 0, 256),), 6)
+        open_sum("31", ((3, 256, 256),), 7)
+        round_z("20")
+        take("30", 0, sbuf("taken30", [P, 256], F32)[:])
+        round_z("30")
+        take("31", 0, sbuf("taken31", [P, 256], F32)[:])
+        round_z("31")
+        open_sum("A0", ((2, 512, 256),), 5)
+        take("A0", 0, sbuf("taken20", [P, 256], F32)[:])
+        turn_back(0, 256, 4, True)
+        turn_back(256, 256, 6, True)
+        round_z("A0")
+        open_sum("A1", ((3, 512, 256),), 1)
+        take("A1", 0, sbuf("taken30", [P, 256], F32)[:])
+        round_z("A1")
+        open_sum("B", ((1, 768, 256), (2, 768, 256)), 0)
+        open_sum("C", ((3, 768, 128),), 2)
+        open_sum("D", ((3, 896, 128),), 3)
+        take("B", 0, sbuf("taken31", [P, 256], F32)[:])
+        take("B", 1, sbuf("taken20", [P, 256], F32)[:])
+        round_z("B")
+        late = sbuf("taken30", [P, 256], F32)
+        turn_back(512, 256, 7, False)
+        take("C", 0, late[:, 0:128])
+        take("D", 0, late[:, 128:256])
+        round_z("C")
+        round_z("D")
+        quantize_z(0, 256)
+        quantize_z(256, 256)
+        turn_back(768, 128, 4, True)
+        turn_back(896, 128, 1, True)
+        second_layer(0, 5)
+        quantize_z(512, 256)
+        second_layer(1, 6)
+        store(0, True, "result0")
+        quantize_z(768, 128)
+        second_layer(2, 0)
+        quantize_z(896, 128)
+        second_layer(3, 2)
+        store(1, False, "result1")
+        store(2, True, "result2")
+        store(3, False, "result3")

@@ -26,7 +26,7 @@ LIST_ROWS = 16
 HALF = S // 2
 
 W1_LOADS = ((0, 1), (1, 2), (2, 4))
-STEPS = ((0, 512), (512, 256), (768, 128), (896, 128))
+STEPS = ((0, 256), (256, 256), (512, 256), (768, 128), (896, 128))
 PAIR_NODES = 256
 
 
@@ -159,9 +159,23 @@ def tile_picked_treeup_gelu_p_kernel(
         def turn(bank, block, src, start, stop):
             nc.tensor.matmul(bank[:, block, :], lhsT=src, rhs=ident[:], is_transpose=True, start=start, stop=stop)
 
-        def open_sum(name, members, number):
+        def keep_clock_up(bank):
+            nc.tensor.matmul_mx(
+                bank[:],
+                lhsT=w2_codes[:].bitcast(FP8X4),
+                lhsT_scale=w2_plane[:],
+                rhs=x_codes[0, 0][:].bitcast(FP8X4),
+                rhs_scale=x_plane[:, 0:HALF],
+                start=True,
+                stop=True,
+            )
+
+        def open_sum(name, members, number, warm=False):
             blocks = [(c, j) for c, j0, w in members for j in range(j0, j0 + w, P)]
-            bank = bank_tile(number, [P, len(blocks), P])
+            whole = bank_tile(number, [P, HALF])
+            if warm:
+                keep_clock_up(whole)
+            bank = whole[:].rearrange("j (b i) -> j b i", i=P)
             sums[name] = (members, blocks, bank)
             for b, (c, j) in enumerate(blocks):
                 turn(bank, b, h[c][:, j : j + P], b == 0, False)
@@ -200,10 +214,13 @@ def tile_picked_treeup_gelu_p_kernel(
         z_bf = {}
         acc = {}
 
-        def turn_back(j0, w, number, on_scalar):
+        def turn_back(j0, w, number, on_scalar, warm=False):
             pairs = z_rows[:].bitcast(F32)
             blocks = w // P
-            bank = bank_tile(number, [P, blocks, 2, P])
+            whole = bank_tile(number, [P, HALF])
+            if warm:
+                keep_clock_up(whole)
+            bank = whole[:, 0 : 2 * w].rearrange("p (b u j) -> p b u j", u=2, j=P)
             for b in range(blocks):
                 for u in range(2):
                     word0 = 2 * (j0 + P * b) + P * u
@@ -212,7 +229,7 @@ def tile_picked_treeup_gelu_p_kernel(
             copy(
                 on_scalar,
                 z_bf[j0][:].bitcast(F32).rearrange("p (b j u) -> p b j u", b=blocks, u=2),
-                bank[:].rearrange("p b u j -> p b j u"),
+                bank.rearrange("p b u j -> p b j u"),
             )
 
         z_codes = sbuf("z_codes", [P, S], U32)
@@ -303,7 +320,7 @@ def tile_picked_treeup_gelu_p_kernel(
         take("10", 0, sbuf("taken10", [P, HALF], F32)[:])
         open_sum("12", ((1, 512, 256),), 3)
         take("12", 0, sbuf("taken12", [P, 256], F32)[:])
-        open_sum("20", ((2, 0, HALF),), 4)
+        open_sum("20", ((2, 0, HALF),), 4, True)
         round_z("10")
         round_z("12")
         take("20", 0, sbuf("taken20", [P, HALF], F32)[:])
@@ -314,7 +331,7 @@ def tile_picked_treeup_gelu_p_kernel(
         round_z("30")
         take("31", 0, sbuf("taken31", [P, 256], F32)[:])
         round_z("31")
-        open_sum("A0", ((2, 512, 256),), 5)
+        open_sum("A0", ((2, 512, 256),), 5, True)
         take("A0", 0, sbuf("taken20", [P, 256], F32)[:])
         turn_back(0, 256, 4, True)
         turn_back(256, 256, 6, True)
@@ -322,7 +339,7 @@ def tile_picked_treeup_gelu_p_kernel(
         open_sum("A1", ((3, 512, 256),), 1)
         take("A1", 0, sbuf("taken30", [P, 256], F32)[:])
         round_z("A1")
-        open_sum("B", ((1, 768, 256), (2, 768, 256)), 0)
+        open_sum("B", ((1, 768, 256), (2, 768, 256)), 0, True)
         open_sum("C", ((3, 768, 128),), 2)
         open_sum("D", ((3, 896, 128),), 3)
         take("B", 0, sbuf("taken31", [P, 256], F32)[:])
@@ -335,17 +352,19 @@ def tile_picked_treeup_gelu_p_kernel(
         round_z("C")
         round_z("D")
         quantize_z(0, 256)
+        second_layer(0, 5)
+        store(0, True, "result0")
         quantize_z(256, 256)
+        second_layer(1, 6)
         turn_back(768, 128, 4, True)
         turn_back(896, 128, 1, True)
-        second_layer(0, 5)
+        store(1, True, "result1")
         quantize_z(512, 256)
-        second_layer(1, 6)
-        store(0, True, "result0")
-        quantize_z(768, 128)
         second_layer(2, 0)
-        quantize_z(896, 128)
+        quantize_z(768, 128)
         second_layer(3, 2)
-        store(1, False, "result1")
+        quantize_z(896, 128)
+        second_layer(4, 3)
         store(2, True, "result2")
         store(3, False, "result3")
+        store(4, True, "result4")

@@ -55,8 +55,8 @@ def tile_picked_treeup_gelu_p_kernel(
         x_table = [sbuf("x_table%d" % g, [P, T], U32) for g in range(PASSES)]
         x_scale_table = sbuf("x_scale_table", [P, T], U8)
         w1_raw = [[sbuf("w1_raw%d_%d" % (lo, g), [P, PACK, P * (hi - lo)], F32) for g in range(PASSES)] for lo, hi in W1_LOADS]
-        share_sb = [sbuf("share%d" % a, [P, HALF], F32) for a in range(2)]
-        share_cols = sbuf("share_cols", [P, 2, HALF // P], F32)
+        share_sb = sbuf("share_sb", [P, S], F32)
+        share_cols = sbuf("share_cols", [P, S // P], F32)
         w2_codes = sbuf("w2_codes", [P, N], U32)
         w2_plane = sbuf("w2_plane", [P, N], U8)
         ident = sbuf("ident", [P, P], F32)
@@ -79,7 +79,7 @@ def tile_picked_treeup_gelu_p_kernel(
             )
 
         nc.sync.dma_start(offs_sb[:], offs)
-        nc.sync.dma_start(out=share_cols[:], in_=share[0].rearrange("(a p b) -> p a b", a=2, b=HALF // P))
+        nc.sync.dma_start(out=share_cols[:], in_=share[0].rearrange("(p b) -> p b", p=P))
         load_x(0, 0, T // 4)
         for quad in range(QUADRANTS):
             nc.sync.dma_start(
@@ -106,8 +106,8 @@ def tile_picked_treeup_gelu_p_kernel(
         def list_slice(list_sb, first, count):
             return list_sb[:, first // LIST_ROWS : (first + count) // LIST_ROWS]
 
-        def gather_x(dst, g, j0, width):
-            nc.vector.tensor_copy(dst, x_table[g][:].indirect(list_slice(offs_sb, j0, width)))
+        def gather_x(g, j0, width):
+            nc.vector.tensor_copy(x_codes[g][:, j0 : j0 + width], x_table[g][:].indirect(list_slice(offs_sb, j0, width)))
 
         w1_bf = [[sbuf("w1_bf%d_%d" % (c, g), [P, P, PACK], BF16) for g in range(PASSES)] for c in range(CHUNKS)]
         w1_codes = [[sbuf("w1_codes%d_%d" % (c, g), [P, P], U32) for g in range(PASSES)] for c in range(CHUNKS)]
@@ -138,12 +138,11 @@ def tile_picked_treeup_gelu_p_kernel(
 
         def product_pass(c, g):
             for j0, w, bank in u_banks[c]:
-                a = j0 // HALF
                 nc.tensor.matmul_mx(
                     bank[:],
                     lhsT=w1_codes[c][g][:].bitcast(FP8X4),
                     lhsT_scale=w1_plane[c][g][:],
-                    rhs=x_codes[g, a][:, j0 - HALF * a : j0 - HALF * a + w].bitcast(FP8X4),
+                    rhs=x_codes[g][:, j0 : j0 + w].bitcast(FP8X4),
                     rhs_scale=x_plane[4 * g : P, j0 : j0 + w],
                     start=(g == 0),
                     stop=(g == PASSES - 1),
@@ -159,22 +158,22 @@ def tile_picked_treeup_gelu_p_kernel(
         def turn(bank, block, src, start, stop):
             nc.tensor.matmul(bank[:, block, :], lhsT=src, rhs=ident[:], is_transpose=True, start=start, stop=stop)
 
-        def keep_clock_up(bank):
+        def keep_clock_up(bank, width):
             nc.tensor.matmul_mx(
-                bank[:],
+                bank[:, 0:width],
                 lhsT=w2_codes[:].bitcast(FP8X4),
                 lhsT_scale=w2_plane[:],
-                rhs=x_codes[0, 0][:].bitcast(FP8X4),
-                rhs_scale=x_plane[:, 0:HALF],
+                rhs=x_codes[0][:, 0:width].bitcast(FP8X4),
+                rhs_scale=x_plane[:, 0:width],
                 start=True,
                 stop=True,
             )
 
-        def open_sum(name, members, number, warm=False):
+        def open_sum(name, members, number, warm=0):
             blocks = [(c, j) for c, j0, w in members for j in range(j0, j0 + w, P)]
             whole = bank_tile(number, [P, HALF])
             if warm:
-                keep_clock_up(whole)
+                keep_clock_up(whole, warm)
             bank = whole[:].rearrange("j (b i) -> j b i", i=P)
             sums[name] = (members, blocks, bank)
             for b, (c, j) in enumerate(blocks):
@@ -182,11 +181,10 @@ def tile_picked_treeup_gelu_p_kernel(
 
         def gather_h(name, member, taken):
             c, j0, w = sums[name][0][member]
-            a = j0 // HALF
             nc.vector.tensor_tensor(
                 taken,
                 h[c][:].indirect(list_slice(par_sb, j0, w)),
-                share_sb[a][:, j0 - HALF * a : j0 - HALF * a + w],
+                share_sb[:, j0 : j0 + w],
                 MULT,
             )
 
@@ -214,12 +212,12 @@ def tile_picked_treeup_gelu_p_kernel(
         z_bf = {}
         acc = {}
 
-        def turn_back(j0, w, number, on_scalar, warm=False):
+        def turn_back(j0, w, number, on_scalar, warm=0):
             pairs = z_rows[:].bitcast(F32)
             blocks = w // P
             whole = bank_tile(number, [P, HALF])
             if warm:
-                keep_clock_up(whole)
+                keep_clock_up(whole, warm)
             bank = whole[:, 0 : 2 * w].rearrange("p (b u j) -> p b u j", u=2, j=P)
             for b in range(blocks):
                 for u in range(2):
@@ -261,22 +259,21 @@ def tile_picked_treeup_gelu_p_kernel(
 
         x_plane = sbuf("x_plane", [P, S], U8)
         nc.vector.tensor_copy(x_plane[:], x_scale_table[:].indirect(offs_sb[:]))
-        for a in range(2):
-            x_codes[0, a] = sbuf("x_codes0_%d" % a, [P, HALF], U32)
-            gather_x(x_codes[0, a][:], 0, HALF * a, HALF)
+        x_codes[0] = sbuf("x_codes0", [P, S], U32)
+        gather_x(0, 0, S)
         for g in range(PASSES):
             cast_w1(0, g, True)
             quantize_w1(0, g)
         for a in range(2):
             bank = bank_tile(6 + a, [P, HALF // P, P])
             for b in range(HALF // P):
-                nc.tensor.transpose(bank[:, b, :], share_cols[:, a, b : b + 1].to_broadcast([P, P]), ident[:])
-            nc.scalar.copy(share_sb[a][:].rearrange("m (n b) -> m n b", b=HALF // P), bank[:].rearrange("m b n -> m n b"))
-        x_codes[1, 0] = sbuf("x_codes1_0", [P, HALF], U32)
-        gather_x(x_codes[1, 0][:], 1, 0, HALF)
-        x_codes[1, 1] = sbuf("x_codes1_1", [P, HALF], U32)
-        for part in range(2):
-            gather_x(x_codes[1, 1][:, 256 * part : 256 * (part + 1)], 1, HALF + 256 * part, 256)
+                nc.tensor.transpose(bank[:, b, :], share_cols[:, 4 * a + b : 4 * a + b + 1].to_broadcast([P, P]), ident[:])
+            nc.scalar.copy(
+                share_sb[:].rearrange("m (n b) -> m n b", n=P)[:, :, 4 * a : 4 * a + 4], bank[:].rearrange("m b n -> m n b")
+            )
+        x_codes[1] = sbuf("x_codes1", [P, S], U32)
+        for j0, w in ((0, 512), (512, 256), (768, 256)):
+            gather_x(1, j0, w)
         cast_w1(1, 0, True)
         open_products(0, ((0, 512, 0), (512, 256, 1), (768, 256, 7)))
         for g in range(PASSES):
@@ -287,84 +284,87 @@ def tile_picked_treeup_gelu_p_kernel(
         cast_w1(1, 1, False)
         for g in range(PASSES):
             quantize_w1(1, g)
-        open_products(1, ((0, HALF, 2), (HALF, HALF, 3)))
+        open_products(1, ((0, HALF, 1), (HALF, HALF, 7)))
         for g in range(PASSES):
             product_pass(1, g)
         for c in (2, 3):
             cast_w1(c, 0, True)
         open_sum("00", ((0, 0, HALF),), 0)
-        open_sum("01", ((0, HALF, HALF),), 1)
+        open_sum("01", ((0, HALF, HALF),), 2)
         take("00", 0, sbuf("taken00", [P, HALF], F32)[:])
         for c in (2, 3):
             quantize_w1(c, 0)
-            open_products(c, ((0, HALF, 2 * c), (HALF, HALF, 2 * c + 1)))
+            open_products(c, ((0, HALF, 2 * c), (HALF, HALF, (5, 3)[c - 2])))
             product_pass(c, 0)
-        taken01 = sbuf("w1_raw2_0", [P, HALF], F32)
+        cast_w1(2, 1, False)
+        quantize_w1(2, 1)
+        product_pass(2, 1)
+        taken01 = sbuf("w1_bf3_0", [P, HALF], F32)
         gather_h("01", 0, taken01[:])
         for c in range(1, CHUNKS):
             h[c] = sbuf("h%d" % c, [P, S], F32)
         gelu(1, 0)
         cast_w1(3, 1, True)
         gelu(1, 1)
-        cast_w1(2, 1, False)
-        for c in (2, 3):
-            quantize_w1(c, 1)
-            product_pass(c, 1)
+        quantize_w1(3, 1)
+        product_pass(3, 1)
         add_taken("01", 0, taken01[:])
         for c in (2, 3):
             for piece in range(2):
                 gelu(c, piece)
         round_z("00")
         round_z("01")
-        open_sum("10", ((1, 0, HALF),), 2)
+        open_sum("10", ((1, 0, HALF),), 1)
         take("10", 0, sbuf("taken10", [P, HALF], F32)[:])
-        open_sum("12", ((1, 512, 256),), 3)
+        open_sum("12", ((1, 512, 256),), 7)
         take("12", 0, sbuf("taken12", [P, 256], F32)[:])
-        open_sum("20", ((2, 0, HALF),), 4, True)
+        open_sum("20", ((2, 0, HALF),), 4)
+        open_sum("A0", ((2, 512, 256),), 5, 512)
         round_z("10")
         round_z("12")
         take("20", 0, sbuf("taken20", [P, HALF], F32)[:])
         open_sum("30", ((3, 0, 256),), 6)
-        open_sum("31", ((3, 256, 256),), 7)
+        open_sum("31", ((3, 256, 256),), 3)
         round_z("20")
         take("30", 0, sbuf("taken30", [P, 256], F32)[:])
         round_z("30")
+        open_sum("B0", ((1, 768, 256),), 0)
         take("31", 0, sbuf("taken31", [P, 256], F32)[:])
         round_z("31")
-        open_sum("A0", ((2, 512, 256),), 5, True)
+        open_sum("A1", ((3, 512, 256),), 2, 512)
         take("A0", 0, sbuf("taken20", [P, 256], F32)[:])
         turn_back(0, 256, 4, True)
         turn_back(256, 256, 6, True)
         round_z("A0")
-        open_sum("A1", ((3, 512, 256),), 1)
         take("A1", 0, sbuf("taken30", [P, 256], F32)[:])
         round_z("A1")
-        open_sum("B", ((1, 768, 256), (2, 768, 256)), 0, True)
-        open_sum("C", ((3, 768, 128),), 2)
-        open_sum("D", ((3, 896, 128),), 3)
-        take("B", 0, sbuf("taken31", [P, 256], F32)[:])
-        take("B", 1, sbuf("taken20", [P, 256], F32)[:])
-        round_z("B")
+        take("B0", 0, sbuf("taken31", [P, 256], F32)[:])
+        round_z("B0")
+        open_sum("B1", ((2, 768, 256),), 5, 512)
+        open_sum("C", ((3, 768, 128),), 1)
+        open_sum("D", ((3, 896, 128),), 7)
+        take("B1", 0, sbuf("taken20", [P, 256], F32)[:])
+        round_z("B1")
         late = sbuf("taken30", [P, 256], F32)
-        turn_back(512, 256, 7, False)
+        turn_back(512, 256, 3, False)
         take("C", 0, late[:, 0:128])
         take("D", 0, late[:, 128:256])
         round_z("C")
         round_z("D")
         quantize_z(0, 256)
-        second_layer(0, 5)
+        second_layer(0, 0)
         store(0, True, "result0")
         quantize_z(256, 256)
         second_layer(1, 6)
         turn_back(768, 128, 4, True)
-        turn_back(896, 128, 1, True)
+        turn_back(896, 128, 2, True)
         store(1, True, "result1")
         quantize_z(512, 256)
-        second_layer(2, 0)
+        second_layer(2, 5)
         quantize_z(768, 128)
-        second_layer(3, 2)
+        second_layer(3, 1)
         quantize_z(896, 128)
-        second_layer(4, 3)
+        second_layer(4, 7)
         store(2, True, "result2")
         store(3, False, "result3")
         store(4, True, "result4")

@@ -24,10 +24,15 @@ CHUNKS = H // P
 QUADRANTS = 4
 LIST_ROWS = 16
 HALF = S // 2
+QUARTER = S // 4
 
-W1_LOADS = ((0, 1), (1, 2), (2, 4))
-STEPS = ((0, 256), (256, 256), (512, 256), (768, 128), (896, 128))
-PAIR_NODES = 256
+PIECES = (
+    ((0, HALF, 0), (HALF, QUARTER, 1), (HALF + QUARTER, QUARTER, 7)),
+    ((0, HALF, 1), (HALF, HALF, 7)),
+    ((0, HALF, 4), (HALF, HALF, 5)),
+    ((0, HALF, 6), (HALF, HALF, 3)),
+)
+STEPS = ((0, QUARTER), (QUARTER, QUARTER), (HALF, QUARTER), (HALF + QUARTER, P), (S - P, P))
 
 
 def tile_picked_treeup_gelu_p_kernel(
@@ -54,7 +59,7 @@ def tile_picked_treeup_gelu_p_kernel(
         par_sb = keep.tile([P, S // LIST_ROWS], U16, name="par_sb")
         x_table = [sbuf("x_table%d" % g, [P, T], U32) for g in range(PASSES)]
         x_scale_table = sbuf("x_scale_table", [P, T], U8)
-        w1_raw = [[sbuf("w1_raw%d_%d" % (lo, g), [P, PACK, P * (hi - lo)], F32) for g in range(PASSES)] for lo, hi in W1_LOADS]
+        w1_raw = [[sbuf("w1_raw%d_%d" % (c, g), [P, PACK, P], F32) for g in range(PASSES)] for c in range(CHUNKS)]
         share_sb = sbuf("share_sb", [P, S], F32)
         share_cols = sbuf("share_cols", [P, S // P], F32)
         w2_codes = sbuf("w2_codes", [P, N], U32)
@@ -71,12 +76,12 @@ def tile_picked_treeup_gelu_p_kernel(
             words = x_words[g].rearrange("p n t -> p (n t)").bitcast(I32)
             nc.sync.dma_start(out=x_table[g][:, lo:hi].bitcast(I32), in_=words[:, lo:hi])
 
-        def load_w1(load, g):
-            lo, hi = W1_LOADS[load]
-            nc.sync.dma_start(
-                out=w1_raw[load][g][:],
-                in_=w1[PASS * g : PASS * (g + 1), P * lo : P * hi].rearrange("(p r) m -> p r m", r=PACK),
-            )
+        def load_w1(c):
+            for g in range(PASSES):
+                nc.sync.dma_start(
+                    out=w1_raw[c][g][:],
+                    in_=w1[PASS * g : PASS * (g + 1), P * c : P * (c + 1)].rearrange("(p r) m -> p r m", r=PACK),
+                )
 
         nc.sync.dma_start(offs_sb[:], offs)
         nc.sync.dma_start(out=share_cols[:], in_=share[0].rearrange("(p b) -> p b", p=P))
@@ -87,13 +92,11 @@ def tile_picked_treeup_gelu_p_kernel(
                 in_=x_scales[:, 4 * quad : 4 * quad + 4, :].bitcast(I32),
             )
         load_x(0, T // 4, T)
-        load_w1(0, 0)
-        load_w1(0, 1)
+        load_w1(0)
         load_x(1, 0, T)
         nc.sync.dma_start(par_sb[:], par)
-        for load in range(1, len(W1_LOADS)):
-            for g in range(PASSES):
-                load_w1(load, g)
+        for c in range(1, CHUNKS):
+            load_w1(c)
         make_identity(nc, ident[:])
         nc.gpsimd.memset(w2_plane[:], 0)
         nc.sync.dma_start(out=w2_codes[:].bitcast(I32), in_=w2_words[0].rearrange("p n t -> p (n t)").bitcast(I32))
@@ -113,13 +116,11 @@ def tile_picked_treeup_gelu_p_kernel(
         w1_codes = [[sbuf("w1_codes%d_%d" % (c, g), [P, P], U32) for g in range(PASSES)] for c in range(CHUNKS)]
         w1_plane = [[sbuf("w1_plane%d_%d" % (c, g), [P, P], U8) for g in range(PASSES)] for c in range(CHUNKS)]
 
-        def cast_w1(c, g, on_scalar):
-            load = [number for number, (lo, hi) in enumerate(W1_LOADS) if lo <= c < hi][0]
-            m0 = P * (c - W1_LOADS[load][0])
+        def cast_w1(c, g, on_scalar=True):
             copy(
                 on_scalar,
                 w1_bf[c][g][:].rearrange("p (m n) r -> p m r n", n=4),
-                w1_raw[load][g][:, :, m0 : m0 + P].rearrange("p r (m n) -> p m r n", n=4),
+                w1_raw[c][g][:].rearrange("p r (m n) -> p m r n", n=4),
             )
 
         def quantize_w1(c, g):
@@ -131,240 +132,223 @@ def tile_picked_treeup_gelu_p_kernel(
 
         x_codes = {}
         h = {}
-        u_banks = {}
+        products = {}
 
-        def open_products(c, pieces):
-            u_banks[c] = [(j0, w, bank_tile(number, [P, w])) for j0, w, number in pieces]
+        def open_products(c):
+            products[c] = [(j0, width, bank_tile(number, [P, width])) for j0, width, number in PIECES[c]]
 
         def product_pass(c, g):
-            for j0, w, bank in u_banks[c]:
+            for j0, width, bank in products[c]:
                 nc.tensor.matmul_mx(
                     bank[:],
                     lhsT=w1_codes[c][g][:].bitcast(FP8X4),
                     lhsT_scale=w1_plane[c][g][:],
-                    rhs=x_codes[g][:, j0 : j0 + w].bitcast(FP8X4),
-                    rhs_scale=x_plane[4 * g : P, j0 : j0 + w],
+                    rhs=x_codes[g][:, j0 : j0 + width].bitcast(FP8X4),
+                    rhs_scale=x_plane[4 * g : P, j0 : j0 + width],
                     start=(g == 0),
                     stop=(g == PASSES - 1),
                 )
 
         def gelu(c, piece):
-            j0, w, bank = u_banks[c][piece]
-            nc.scalar.activation(h[c][:, j0 : j0 + w], bank[:], GELU)
+            j0, width, bank = products[c][piece]
+            nc.scalar.activation(h[c][:, j0 : j0 + width], bank[:], GELU)
 
         z_rows = sbuf("z_rows", [P, PACK * S], BF16)
         sums = {}
 
-        def turn(bank, block, src, start, stop):
-            nc.tensor.matmul(bank[:, block, :], lhsT=src, rhs=ident[:], is_transpose=True, start=start, stop=stop)
-
-        def keep_clock_up(bank, width):
-            nc.tensor.matmul_mx(
-                bank[:, 0:width],
-                lhsT=w2_codes[:].bitcast(FP8X4),
-                lhsT_scale=w2_plane[:],
-                rhs=x_codes[0][:, 0:width].bitcast(FP8X4),
-                rhs_scale=x_plane[:, 0:width],
-                start=True,
-                stop=True,
-            )
-
-        def open_sum(name, members, number, warm=0):
-            blocks = [(c, j) for c, j0, w in members for j in range(j0, j0 + w, P)]
+        def open_sum(c, j0, width, number, warm_up=False):
             whole = bank_tile(number, [P, HALF])
-            if warm:
-                keep_clock_up(whole, warm)
-            bank = whole[:].rearrange("j (b i) -> j b i", i=P)
-            sums[name] = (members, blocks, bank)
-            for b, (c, j) in enumerate(blocks):
-                turn(bank, b, h[c][:, j : j + P], b == 0, False)
-
-        def gather_h(name, member, taken):
-            c, j0, w = sums[name][0][member]
-            nc.vector.tensor_tensor(
-                taken,
-                h[c][:].indirect(list_slice(par_sb, j0, w)),
-                share_sb[:, j0 : j0 + w],
-                MULT,
-            )
-
-        def add_taken(name, member, taken):
-            members, blocks, bank = sums[name]
-            c, j0, w = members[member]
-            for j in range(j0, j0 + w, P):
-                b = blocks.index((c, j))
-                turn(bank, b, taken[:, j - j0 : j - j0 + P], False, b == len(blocks) - 1)
-
-        def take(name, member, taken):
-            gather_h(name, member, taken)
-            add_taken(name, member, taken)
-
-        def round_z(name):
-            members, blocks, bank = sums[name]
-            rows = z_rows[:].rearrange("j (b u p e) -> j b u p e", u=2, p=P, e=2)
-            for c, j0, width in members:
-                b0 = blocks.index((c, j0))
-                nc.scalar.copy(
-                    rows[:, j0 // P : (j0 + width) // P, :, 32 * c : 32 * (c + 1), :],
-                    bank[:, b0 : b0 + width // P, :].rearrange("j b (p u e) -> j b u p e", u=2, e=2),
+            if warm_up:
+                nc.tensor.matmul_mx(
+                    whole[:],
+                    lhsT=w2_codes[:].bitcast(FP8X4),
+                    lhsT_scale=w2_plane[:],
+                    rhs=x_codes[0][:, 0:HALF].bitcast(FP8X4),
+                    rhs_scale=x_plane[:, 0:HALF],
+                    start=True,
+                    stop=True,
                 )
+            bank = whole[:].rearrange("j (b i) -> j b i", i=P)
+            sums[c, j0] = (width, bank)
+            for b in range(width // P):
+                src = h[c][:, j0 + P * b : j0 + P * (b + 1)]
+                nc.tensor.matmul(bank[:, b, :], lhsT=src, rhs=ident[:], is_transpose=True, start=(b == 0), stop=False)
+
+        def gather_h(c, j0, taken):
+            width = sums[c, j0][0]
+            nc.vector.tensor_tensor(taken, h[c][:].indirect(list_slice(par_sb, j0, width)), share_sb[:, j0 : j0 + width], MULT)
+
+        def add_taken(c, j0, taken):
+            width, bank = sums[c, j0]
+            blocks = width // P
+            for b in range(blocks):
+                src = taken[:, P * b : P * (b + 1)]
+                nc.tensor.matmul(bank[:, b, :], lhsT=src, rhs=ident[:], is_transpose=True, start=False, stop=(b == blocks - 1))
+
+        def take(c, j0, tag):
+            taken = sbuf(tag, [P, sums[c, j0][0]], F32)
+            gather_h(c, j0, taken[:])
+            add_taken(c, j0, taken[:])
+
+        def round_z(c, j0):
+            width, bank = sums[c, j0]
+            rows = z_rows[:].rearrange("j (b u p e) -> j b u p e", u=2, p=P, e=2)
+            nc.scalar.copy(
+                rows[:, j0 // P : (j0 + width) // P, :, 32 * c : 32 * (c + 1), :],
+                bank[:, 0 : width // P, :].rearrange("j b (p u e) -> j b u p e", u=2, e=2),
+            )
 
         z_bf = {}
         acc = {}
 
-        def turn_back(j0, w, number, on_scalar, warm=0):
+        def turn_back(step, number, on_scalar=True):
+            j0, width = STEPS[step]
             pairs = z_rows[:].bitcast(F32)
-            blocks = w // P
+            blocks = width // P
             whole = bank_tile(number, [P, HALF])
-            if warm:
-                keep_clock_up(whole, warm)
-            bank = whole[:, 0 : 2 * w].rearrange("p (b u j) -> p b u j", u=2, j=P)
+            bank = whole[:, 0 : 2 * width].rearrange("p (b u j) -> p b u j", u=2, j=P)
             for b in range(blocks):
                 for u in range(2):
                     word0 = 2 * (j0 + P * b) + P * u
                     nc.tensor.transpose(bank[:, b, u, :], pairs[:, word0 : word0 + P], ident[:])
-            z_bf[j0] = sbuf("z_bf%d" % j0, [P, PACK * w], BF16)
+            z_bf[step] = sbuf("z_bf%d" % step, [P, PACK * width], BF16)
             copy(
                 on_scalar,
-                z_bf[j0][:].bitcast(F32).rearrange("p (b j u) -> p b j u", b=blocks, u=2),
+                z_bf[step][:].bitcast(F32).rearrange("p (b j u) -> p b j u", b=blocks, u=2),
                 bank.rearrange("p b u j -> p b j u"),
             )
 
         z_codes = sbuf("z_codes", [P, S], U32)
         z_plane = sbuf("z_plane", [P, S], U8)
 
-        def quantize_z(j0, w):
-            nc.vector.quantize_mx(
-                out=z_codes[:, j0 : j0 + w].bitcast(FP8X4), scales=z_plane[:, j0 : j0 + w], in_=z_bf[j0][:]
-            )
-
-        def second_layer(s, number):
-            j0, w = STEPS[s]
-            acc[s] = bank_tile(number, [P, w])
+        def second_layer(step, number):
+            j0, width = STEPS[step]
+            codes = z_codes[:, j0 : j0 + width].bitcast(FP8X4)
+            plane = z_plane[:, j0 : j0 + width]
+            nc.vector.quantize_mx(out=codes, scales=plane, in_=z_bf[step][:])
+            acc[step] = bank_tile(number, [P, width])
             nc.tensor.matmul_mx(
-                acc[s][:],
+                acc[step][:],
                 lhsT=w2_codes[:].bitcast(FP8X4),
                 lhsT_scale=w2_plane[:],
-                rhs=z_codes[:, j0 : j0 + w].bitcast(FP8X4),
-                rhs_scale=z_plane[:, j0 : j0 + w],
+                rhs=codes,
+                rhs_scale=plane,
                 start=True,
                 stop=True,
             )
 
-        def store(s, on_scalar, tag):
-            j0, w = STEPS[s]
-            result = sbuf(tag, [P, w], F32)
-            copy(on_scalar, result[:], acc[s][:])
-            nc.sync.dma_start(out=out[:, j0 : j0 + w], in_=result[:])
+        def store(step, on_scalar=True):
+            j0, width = STEPS[step]
+            result = sbuf("result%d" % step, [P, width], F32)
+            copy(on_scalar, result[:], acc[step][:])
+            nc.sync.dma_start(out=out[:, j0 : j0 + width], in_=result[:])
 
         x_plane = sbuf("x_plane", [P, S], U8)
         nc.vector.tensor_copy(x_plane[:], x_scale_table[:].indirect(offs_sb[:]))
         x_codes[0] = sbuf("x_codes0", [P, S], U32)
         gather_x(0, 0, S)
         for g in range(PASSES):
-            cast_w1(0, g, True)
+            cast_w1(0, g)
             quantize_w1(0, g)
         for a in range(2):
-            bank = bank_tile(6 + a, [P, HALF // P, P])
-            for b in range(HALF // P):
+            bank = bank_tile(6 + a, [P, 4, P])
+            for b in range(4):
                 nc.tensor.transpose(bank[:, b, :], share_cols[:, 4 * a + b : 4 * a + b + 1].to_broadcast([P, P]), ident[:])
             nc.scalar.copy(
                 share_sb[:].rearrange("m (n b) -> m n b", n=P)[:, :, 4 * a : 4 * a + 4], bank[:].rearrange("m b n -> m n b")
             )
         x_codes[1] = sbuf("x_codes1", [P, S], U32)
-        for j0, w in ((0, 512), (512, 256), (768, 256)):
-            gather_x(1, j0, w)
-        cast_w1(1, 0, True)
-        open_products(0, ((0, 512, 0), (512, 256, 1), (768, 256, 7)))
+        for j0, width, number in PIECES[0]:
+            gather_x(1, j0, width)
+        cast_w1(1, 0)
+        open_products(0)
         for g in range(PASSES):
             product_pass(0, g)
         h[0] = sbuf("w1_raw1_0", [P, S], F32)
-        for piece in range(3):
+        for piece in range(len(PIECES[0])):
             gelu(0, piece)
-        cast_w1(1, 1, False)
+
+        cast_w1(1, 1, on_scalar=False)
         for g in range(PASSES):
             quantize_w1(1, g)
-        open_products(1, ((0, HALF, 1), (HALF, HALF, 7)))
+        open_products(1)
         for g in range(PASSES):
             product_pass(1, g)
-        for c in (2, 3):
-            cast_w1(c, 0, True)
-        open_sum("00", ((0, 0, HALF),), 0)
-        open_sum("01", ((0, HALF, HALF),), 2)
-        take("00", 0, sbuf("taken00", [P, HALF], F32)[:])
-        for c in (2, 3):
-            quantize_w1(c, 0)
-            open_products(c, ((0, HALF, 2 * c), (HALF, HALF, (5, 3)[c - 2])))
-            product_pass(c, 0)
-        cast_w1(2, 1, False)
-        quantize_w1(2, 1)
-        product_pass(2, 1)
-        taken01 = sbuf("w1_bf3_0", [P, HALF], F32)
-        gather_h("01", 0, taken01[:])
+        for g in range(PASSES):
+            cast_w1(2, g)
+        open_sum(0, 0, HALF, 0)
+        open_sum(0, HALF, HALF, 2)
+        take(0, 0, "taken_first")
+        open_products(2)
+        for g in range(PASSES):
+            quantize_w1(2, g)
+            product_pass(2, g)
+        taken_second = sbuf("w1_raw2_1", [P, HALF], F32)
+        gather_h(0, HALF, taken_second[:])
         for c in range(1, CHUNKS):
             h[c] = sbuf("h%d" % c, [P, S], F32)
-        gelu(1, 0)
-        cast_w1(3, 1, True)
-        gelu(1, 1)
-        quantize_w1(3, 1)
-        product_pass(3, 1)
-        add_taken("01", 0, taken01[:])
+        open_products(3)
+        for g in range(PASSES):
+            cast_w1(3, g)
+            gelu(1, g)
+            quantize_w1(3, g)
+            product_pass(3, g)
+        add_taken(0, HALF, taken_second[:])
         for c in (2, 3):
-            for piece in range(2):
+            for piece in range(len(PIECES[c])):
                 gelu(c, piece)
-        round_z("00")
-        round_z("01")
-        open_sum("10", ((1, 0, HALF),), 1)
-        take("10", 0, sbuf("taken10", [P, HALF], F32)[:])
-        open_sum("12", ((1, 512, 256),), 7)
-        take("12", 0, sbuf("taken12", [P, 256], F32)[:])
-        open_sum("20", ((2, 0, HALF),), 4)
-        open_sum("A0", ((2, 512, 256),), 5, 512)
-        round_z("10")
-        round_z("12")
-        take("20", 0, sbuf("taken20", [P, HALF], F32)[:])
-        open_sum("30", ((3, 0, 256),), 6)
-        open_sum("31", ((3, 256, 256),), 3)
-        round_z("20")
-        take("30", 0, sbuf("taken30", [P, 256], F32)[:])
-        round_z("30")
-        open_sum("B0", ((1, 768, 256),), 0)
-        take("31", 0, sbuf("taken31", [P, 256], F32)[:])
-        round_z("31")
-        open_sum("A1", ((3, 512, 256),), 2, 512)
-        take("A0", 0, sbuf("taken20", [P, 256], F32)[:])
-        turn_back(0, 256, 4, True)
-        turn_back(256, 256, 6, True)
-        round_z("A0")
-        take("A1", 0, sbuf("taken30", [P, 256], F32)[:])
-        round_z("A1")
-        take("B0", 0, sbuf("taken31", [P, 256], F32)[:])
-        round_z("B0")
-        open_sum("B1", ((2, 768, 256),), 5, 512)
-        open_sum("C", ((3, 768, 128),), 1)
-        open_sum("D", ((3, 896, 128),), 7)
-        take("B1", 0, sbuf("taken20", [P, 256], F32)[:])
-        round_z("B1")
-        late = sbuf("taken30", [P, 256], F32)
-        turn_back(512, 256, 3, False)
-        take("C", 0, late[:, 0:128])
-        take("D", 0, late[:, 128:256])
-        round_z("C")
-        round_z("D")
-        quantize_z(0, 256)
+        round_z(0, 0)
+        round_z(0, HALF)
+
+        third, fourth = HALF, HALF + QUARTER
+        open_sum(1, 0, HALF, 1)
+        take(1, 0, "taken_chunk1")
+        open_sum(1, third, QUARTER, 7)
+        take(1, third, "taken_filler")
+        open_sum(2, 0, HALF, 4)
+        open_sum(2, third, QUARTER, 5, warm_up=True)
+        round_z(1, 0)
+        round_z(1, third)
+        take(2, 0, "stage0")
+        open_sum(3, 0, QUARTER, 6)
+        open_sum(3, QUARTER, QUARTER, 3)
+        round_z(2, 0)
+        take(3, 0, "stage1")
+        round_z(3, 0)
+        open_sum(1, fourth, QUARTER, 0)
+        take(3, QUARTER, "stage2")
+        round_z(3, QUARTER)
+
+        open_sum(3, third, QUARTER, 2, warm_up=True)
+        take(2, third, "stage0")
+        turn_back(0, 4)
+        turn_back(1, 6)
+        round_z(2, third)
+        take(3, third, "stage1")
+        round_z(3, third)
+        take(1, fourth, "stage2")
+        round_z(1, fourth)
+        open_sum(2, fourth, QUARTER, 5, warm_up=True)
+        open_sum(3, fourth, P, 1)
+        open_sum(3, fourth + P, P, 7)
+        take(2, fourth, "stage0")
+        round_z(2, fourth)
+        taken_last = sbuf("stage1", [P, QUARTER], F32)
+        turn_back(2, 3, on_scalar=False)
+        for b in range(2):
+            gather_h(3, fourth + P * b, taken_last[:, P * b : P * (b + 1)])
+            add_taken(3, fourth + P * b, taken_last[:, P * b : P * (b + 1)])
+        for b in range(2):
+            round_z(3, fourth + P * b)
         second_layer(0, 0)
-        store(0, True, "result0")
-        quantize_z(256, 256)
+        store(0)
         second_layer(1, 6)
-        turn_back(768, 128, 4, True)
-        turn_back(896, 128, 2, True)
-        store(1, True, "result1")
-        quantize_z(512, 256)
+        turn_back(3, 4)
+        turn_back(4, 2)
+        store(1)
         second_layer(2, 5)
-        quantize_z(768, 128)
         second_layer(3, 1)
-        quantize_z(896, 128)
         second_layer(4, 7)
-        store(2, True, "result2")
-        store(3, False, "result3")
-        store(4, True, "result4")
+        store(2)
+        store(3, on_scalar=False)
+        store(4)

@@ -28,10 +28,11 @@ QUARTER = S // 4
 
 PIECES = (
     ((0, HALF, 0), (HALF, QUARTER, 1), (HALF + QUARTER, QUARTER, 7)),
+    ((0, HALF, 3), (HALF, HALF, 4)),
+    ((0, HALF, 5), (HALF, HALF, 6)),
     ((0, HALF, 1), (HALF, HALF, 7)),
-    ((0, HALF, 4), (HALF, HALF, 5)),
-    ((0, HALF, 6), (HALF, HALF, 3)),
 )
+SPANS = {(0, 0): 1, (0, 1): 1, (1, 0): 1, (1, 1): 2, (2, 0): 1, (3, 0): 1, (3, 1): 1}
 STEPS = ((0, QUARTER), (QUARTER, QUARTER), (HALF, QUARTER), (HALF + QUARTER, P), (S - P, P))
 
 
@@ -59,8 +60,11 @@ def tile_picked_treeup_gelu_p_kernel(
         par_sb = keep.tile([P, S // LIST_ROWS], U16, name="par_sb")
         x_table = [sbuf("x_table%d" % g, [P, T], U32) for g in range(PASSES)]
         x_scale_table = sbuf("x_scale_table", [P, T], U8)
-        w1_raw = [[sbuf("w1_raw%d_%d" % (c, g), [P, PACK, P], F32) for g in range(PASSES)] for c in range(CHUNKS)]
+        w1_raw = {}
+        for first, g in SPANS:
+            w1_raw[first, g] = sbuf("w1_raw%d_%d" % (first, g), [P, PACK, P * SPANS[first, g]], F32)
         share_sb = sbuf("share_sb", [P, S], F32)
+        share_end = sbuf("share_end", [P, P], F32)
         share_cols = sbuf("share_cols", [P, S // P], F32)
         w2_codes = sbuf("w2_codes", [P, N], U32)
         w2_plane = sbuf("w2_plane", [P, N], U8)
@@ -76,12 +80,12 @@ def tile_picked_treeup_gelu_p_kernel(
             words = x_words[g].rearrange("p n t -> p (n t)").bitcast(I32)
             nc.sync.dma_start(out=x_table[g][:, lo:hi].bitcast(I32), in_=words[:, lo:hi])
 
-        def load_w1(c):
-            for g in range(PASSES):
-                nc.sync.dma_start(
-                    out=w1_raw[c][g][:],
-                    in_=w1[PASS * g : PASS * (g + 1), P * c : P * (c + 1)].rearrange("(p r) m -> p r m", r=PACK),
-                )
+        def load_w1(first, g):
+            columns = slice(P * first, P * (first + SPANS[first, g]))
+            nc.sync.dma_start(
+                out=w1_raw[first, g][:],
+                in_=w1[PASS * g : PASS * (g + 1), columns].rearrange("(p r) m -> p r m", r=PACK),
+            )
 
         nc.sync.dma_start(offs_sb[:], offs)
         nc.sync.dma_start(out=share_cols[:], in_=share[0].rearrange("(p b) -> p b", p=P))
@@ -92,11 +96,15 @@ def tile_picked_treeup_gelu_p_kernel(
                 in_=x_scales[:, 4 * quad : 4 * quad + 4, :].bitcast(I32),
             )
         load_x(0, T // 4, T)
-        load_w1(0)
+        load_w1(0, 0)
+        load_w1(0, 1)
         load_x(1, 0, T)
         nc.sync.dma_start(par_sb[:], par)
-        for c in range(1, CHUNKS):
-            load_w1(c)
+        load_w1(1, 0)
+        load_w1(2, 0)
+        load_w1(1, 1)
+        load_w1(3, 0)
+        load_w1(3, 1)
         make_identity(nc, ident[:])
         nc.gpsimd.memset(w2_plane[:], 0)
         nc.sync.dma_start(out=w2_codes[:].bitcast(I32), in_=w2_words[0].rearrange("p n t -> p (n t)").bitcast(I32))
@@ -112,22 +120,35 @@ def tile_picked_treeup_gelu_p_kernel(
         def gather_x(g, j0, width):
             nc.vector.tensor_copy(x_codes[g][:, j0 : j0 + width], x_table[g][:].indirect(list_slice(offs_sb, j0, width)))
 
-        w1_bf = [[sbuf("w1_bf%d_%d" % (c, g), [P, P, PACK], BF16) for g in range(PASSES)] for c in range(CHUNKS)]
-        w1_codes = [[sbuf("w1_codes%d_%d" % (c, g), [P, P], U32) for g in range(PASSES)] for c in range(CHUNKS)]
-        w1_plane = [[sbuf("w1_plane%d_%d" % (c, g), [P, P], U8) for g in range(PASSES)] for c in range(CHUNKS)]
+        w1_bf = {}
+        w1_codes = {}
+        w1_plane = {}
+        for first, g in SPANS:
+            count = SPANS[first, g]
+            w1_bf[first, g] = sbuf("w1_bf%d_%d" % (first, g), [P, P * count * PACK], BF16)
+            w1_codes[first, g] = sbuf("w1_codes%d_%d" % (first, g), [P, P * count], U32)
+            w1_plane[first, g] = sbuf("w1_plane%d_%d" % (first, g), [P, P * count], U8)
 
-        def cast_w1(c, g, on_scalar=True):
+        def span_of(c, g):
+            first = c if (c, g) in SPANS else c - 1
+            return first, P * (c - first)
+
+        def cast_w1(c, g, on_scalar=True, chunks=1):
+            first, m0 = span_of(c, g)
+            m1 = m0 + P * chunks
             copy(
                 on_scalar,
-                w1_bf[c][g][:].rearrange("p (m n) r -> p m r n", n=4),
-                w1_raw[c][g][:].rearrange("p r (m n) -> p m r n", n=4),
+                w1_bf[first, g][:, PACK * m0 : PACK * m1].rearrange("p (m n r) -> p m r n", n=4, r=PACK),
+                w1_raw[first, g][:, :, m0:m1].rearrange("p r (m n) -> p m r n", n=4),
             )
 
-        def quantize_w1(c, g):
+        def quantize_w1(c, g, chunks=1):
+            first, m0 = span_of(c, g)
+            m1 = m0 + P * chunks
             nc.vector.quantize_mx(
-                out=w1_codes[c][g][:].bitcast(FP8X4),
-                scales=w1_plane[c][g][:],
-                in_=w1_bf[c][g][:].rearrange("p m r -> p (m r)"),
+                out=w1_codes[first, g][:, m0:m1].bitcast(FP8X4),
+                scales=w1_plane[first, g][:, m0:m1],
+                in_=w1_bf[first, g][:, PACK * m0 : PACK * m1],
             )
 
         x_codes = {}
@@ -138,11 +159,12 @@ def tile_picked_treeup_gelu_p_kernel(
             products[c] = [(j0, width, bank_tile(number, [P, width])) for j0, width, number in PIECES[c]]
 
         def product_pass(c, g):
+            first, m0 = span_of(c, g)
             for j0, width, bank in products[c]:
                 nc.tensor.matmul_mx(
                     bank[:],
-                    lhsT=w1_codes[c][g][:].bitcast(FP8X4),
-                    lhsT_scale=w1_plane[c][g][:],
+                    lhsT=w1_codes[first, g][:, m0 : m0 + P].bitcast(FP8X4),
+                    lhsT_scale=w1_plane[first, g][:, m0 : m0 + P],
                     rhs=x_codes[g][:, j0 : j0 + width].bitcast(FP8X4),
                     rhs_scale=x_plane[4 * g : P, j0 : j0 + width],
                     start=(g == 0),
@@ -156,15 +178,15 @@ def tile_picked_treeup_gelu_p_kernel(
         z_rows = sbuf("z_rows", [P, PACK * S], BF16)
         sums = {}
 
-        def open_sum(c, j0, width, number, warm_up=False):
+        def open_sum(c, j0, width, number, warm_up=0):
             whole = bank_tile(number, [P, HALF])
             if warm_up:
                 nc.tensor.matmul_mx(
-                    whole[:],
+                    whole[:, 0:warm_up],
                     lhsT=w2_codes[:].bitcast(FP8X4),
                     lhsT_scale=w2_plane[:],
-                    rhs=x_codes[0][:, 0:HALF].bitcast(FP8X4),
-                    rhs_scale=x_plane[:, 0:HALF],
+                    rhs=x_codes[0][:, 0:warm_up].bitcast(FP8X4),
+                    rhs_scale=x_plane[:, 0:warm_up],
                     start=True,
                     stop=True,
                 )
@@ -176,7 +198,8 @@ def tile_picked_treeup_gelu_p_kernel(
 
         def gather_h(c, j0, taken):
             width = sums[c, j0][0]
-            nc.vector.tensor_tensor(taken, h[c][:].indirect(list_slice(par_sb, j0, width)), share_sb[:, j0 : j0 + width], MULT)
+            factor = share_end[:] if (j0, width) == (S - P, P) else share_sb[:, j0 : j0 + width]
+            nc.vector.tensor_tensor(taken, h[c][:].indirect(list_slice(par_sb, j0, width)), factor, MULT)
 
         def add_taken(c, j0, taken):
             width, bank = sums[c, j0]
@@ -200,6 +223,7 @@ def tile_picked_treeup_gelu_p_kernel(
 
         z_bf = {}
         acc = {}
+        late = {}
 
         def turn_back(step, number, on_scalar=True):
             j0, width = STEPS[step]
@@ -218,12 +242,11 @@ def tile_picked_treeup_gelu_p_kernel(
                 bank.rearrange("p b u j -> p b j u"),
             )
 
-        z_codes = sbuf("z_codes", [P, S], U32)
         z_plane = sbuf("z_plane", [P, S], U8)
 
         def second_layer(step, number):
             j0, width = STEPS[step]
-            codes = z_codes[:, j0 : j0 + width].bitcast(FP8X4)
+            codes = late["z_codes"][:, j0 : j0 + width].bitcast(FP8X4)
             plane = z_plane[:, j0 : j0 + width]
             nc.vector.quantize_mx(out=codes, scales=plane, in_=z_bf[step][:])
             acc[step] = bank_tile(number, [P, width])
@@ -257,10 +280,12 @@ def tile_picked_treeup_gelu_p_kernel(
             nc.scalar.copy(
                 share_sb[:].rearrange("m (n b) -> m n b", n=P)[:, :, 4 * a : 4 * a + 4], bank[:].rearrange("m b n -> m n b")
             )
+        nc.scalar.copy(share_end[:], share_sb[:, S - P : S])
         x_codes[1] = sbuf("x_codes1", [P, S], U32)
         for j0, width, number in PIECES[0]:
             gather_x(1, j0, width)
         cast_w1(1, 0)
+        cast_w1(2, 0)
         open_products(0)
         for g in range(PASSES):
             product_pass(0, g)
@@ -268,87 +293,88 @@ def tile_picked_treeup_gelu_p_kernel(
         for piece in range(len(PIECES[0])):
             gelu(0, piece)
 
-        cast_w1(1, 1, on_scalar=False)
-        for g in range(PASSES):
-            quantize_w1(1, g)
-        open_products(1)
-        for g in range(PASSES):
-            product_pass(1, g)
-        for g in range(PASSES):
-            cast_w1(2, g)
-        open_sum(0, 0, HALF, 0)
-        open_sum(0, HALF, HALF, 2)
-        take(0, 0, "taken_first")
-        open_products(2)
-        for g in range(PASSES):
-            quantize_w1(2, g)
-            product_pass(2, g)
-        taken_second = sbuf("w1_raw2_1", [P, HALF], F32)
-        gather_h(0, HALF, taken_second[:])
+        third, fourth = HALF, HALF + QUARTER
+        for c in (1, 2):
+            quantize_w1(c, 0)
+        for c in (1, 2):
+            cast_w1(c, 1, on_scalar=False)
+        for c in (1, 2):
+            quantize_w1(c, 1)
         for c in range(1, CHUNKS):
             h[c] = sbuf("h%d" % c, [P, S], F32)
-        open_products(3)
+        for c in (1, 2):
+            open_products(c)
+            product_pass(c, 0)
+        for c in (1, 2):
+            product_pass(c, 1)
+        open_sum(0, 0, HALF, 0)
+        open_sum(0, HALF, HALF, 2)
         for g in range(PASSES):
             cast_w1(3, g)
-            gelu(1, g)
+        take(0, 0, "w1_raw1_1")
+        for g in range(PASSES):
             quantize_w1(3, g)
+        open_products(3)
+        for g in range(PASSES):
             product_pass(3, g)
-        add_taken(0, HALF, taken_second[:])
-        for c in (2, 3):
+        for c in (1, 2):
             for piece in range(len(PIECES[c])):
                 gelu(c, piece)
         round_z(0, 0)
+        for piece in range(len(PIECES[3])):
+            gelu(3, piece)
+        take(0, HALF, "w1_raw3_1")
         round_z(0, HALF)
 
-        third, fourth = HALF, HALF + QUARTER
-        open_sum(1, 0, HALF, 1)
+        open_sum(1, 0, HALF, 3)
+        open_sum(1, third, QUARTER, 4)
         take(1, 0, "taken_chunk1")
-        open_sum(1, third, QUARTER, 7)
+        open_sum(2, 0, HALF, 5)
+        open_sum(2, third, QUARTER, 6)
         take(1, third, "taken_filler")
-        open_sum(2, 0, HALF, 4)
-        open_sum(2, third, QUARTER, 5, warm_up=True)
+        open_sum(1, fourth, QUARTER, 0, warm_up=HALF)
         round_z(1, 0)
         round_z(1, third)
         take(2, 0, "stage0")
-        open_sum(3, 0, QUARTER, 6)
-        open_sum(3, QUARTER, QUARTER, 3)
+        open_sum(3, 0, QUARTER, 1)
+        open_sum(3, QUARTER, QUARTER, 7)
         round_z(2, 0)
         take(3, 0, "stage1")
         round_z(3, 0)
-        open_sum(1, fourth, QUARTER, 0)
+        open_sum(3, third, QUARTER, 2)
         take(3, QUARTER, "stage2")
         round_z(3, QUARTER)
 
-        open_sum(3, third, QUARTER, 2, warm_up=True)
+        open_sum(2, fourth, QUARTER, 4, warm_up=HALF)
         take(2, third, "stage0")
-        turn_back(0, 4)
-        turn_back(1, 6)
         round_z(2, third)
+        turn_back(0, 3)
         take(3, third, "stage1")
         round_z(3, third)
+        turn_back(1, 5)
         take(1, fourth, "stage2")
         round_z(1, fourth)
-        open_sum(2, fourth, QUARTER, 5, warm_up=True)
-        open_sum(3, fourth, P, 1)
+        open_sum(3, fourth, P, 1, warm_up=HALF)
         open_sum(3, fourth + P, P, 7)
         take(2, fourth, "stage0")
         round_z(2, fourth)
+        turn_back(2, 6, on_scalar=False)
         taken_last = sbuf("stage1", [P, QUARTER], F32)
-        turn_back(2, 3, on_scalar=False)
         for b in range(2):
             gather_h(3, fourth + P * b, taken_last[:, P * b : P * (b + 1)])
             add_taken(3, fourth + P * b, taken_last[:, P * b : P * (b + 1)])
+        late["z_codes"] = sbuf("share_sb", [P, S], U32)
         for b in range(2):
             round_z(3, fourth + P * b)
-        second_layer(0, 0)
+        second_layer(0, 2)
         store(0)
-        second_layer(1, 6)
-        turn_back(3, 4)
-        turn_back(4, 2)
+        turn_back(3, 3)
+        turn_back(4, 5)
+        second_layer(1, 7)
         store(1)
-        second_layer(2, 5)
-        second_layer(3, 1)
-        second_layer(4, 7)
+        second_layer(2, 0)
+        second_layer(3, 4)
+        second_layer(4, 1)
         store(2)
         store(3, on_scalar=False)
         store(4)

@@ -32,7 +32,7 @@ PIECES = (
     ((0, HALF, 5), (HALF, HALF, 6)),
     ((0, HALF, 1), (HALF, HALF, 7)),
 )
-SPANS = {(0, 0): 1, (0, 1): 1, (1, 0): 1, (1, 1): 2, (2, 0): 1, (3, 0): 1, (3, 1): 1}
+SPANS = {(0, 0): 1, (0, 1): 1, (1, 0): 1, (1, 1): 1, (2, 0): 1, (2, 1): 1, (3, 0): 1, (3, 1): 1}
 STEPS = ((0, QUARTER), (QUARTER, QUARTER), (HALF, QUARTER), (HALF + QUARTER, P), (S - P, P))
 
 
@@ -101,8 +101,9 @@ def tile_picked_treeup_gelu_p_kernel(
         load_x(1, 0, T)
         nc.sync.dma_start(par_sb[:], par)
         load_w1(1, 0)
-        load_w1(2, 0)
         load_w1(1, 1)
+        load_w1(2, 0)
+        load_w1(2, 1)
         load_w1(3, 0)
         load_w1(3, 1)
         make_identity(nc, ident[:])
@@ -158,9 +159,9 @@ def tile_picked_treeup_gelu_p_kernel(
         def open_products(c):
             products[c] = [(j0, width, bank_tile(number, [P, width])) for j0, width, number in PIECES[c]]
 
-        def product_pass(c, g):
+        def product_pass(c, g, pieces=slice(None)):
             first, m0 = span_of(c, g)
-            for j0, width, bank in products[c]:
+            for j0, width, bank in products[c][pieces]:
                 nc.tensor.matmul_mx(
                     bank[:],
                     lhsT=w1_codes[first, g][:, m0 : m0 + P].bitcast(FP8X4),
@@ -213,10 +214,11 @@ def tile_picked_treeup_gelu_p_kernel(
             gather_h(c, j0, taken[:])
             add_taken(c, j0, taken[:])
 
-        def round_z(c, j0):
+        def round_z(c, j0, on_scalar=True):
             width, bank = sums[c, j0]
             rows = z_rows[:].rearrange("j (b u p e) -> j b u p e", u=2, p=P, e=2)
-            nc.scalar.copy(
+            copy(
+                on_scalar,
                 rows[:, j0 // P : (j0 + width) // P, :, 32 * c : 32 * (c + 1), :],
                 bank[:, 0 : width // P, :].rearrange("j b (p u e) -> j b u p e", u=2, e=2),
             )
@@ -284,8 +286,8 @@ def tile_picked_treeup_gelu_p_kernel(
         x_codes[1] = sbuf("x_codes1", [P, S], U32)
         for j0, width, number in PIECES[0]:
             gather_x(1, j0, width)
-        cast_w1(1, 0)
-        cast_w1(2, 0)
+        for g in range(PASSES):
+            cast_w1(1, g)
         open_products(0)
         for g in range(PASSES):
             product_pass(0, g)
@@ -294,44 +296,48 @@ def tile_picked_treeup_gelu_p_kernel(
             gelu(0, piece)
 
         third, fourth = HALF, HALF + QUARTER
-        for c in (1, 2):
-            quantize_w1(c, 0)
-        for c in (1, 2):
-            cast_w1(c, 1, on_scalar=False)
-        for c in (1, 2):
-            quantize_w1(c, 1)
+        quantize_w1(1, 0)
+        cast_w1(2, 0, on_scalar=False)
+        quantize_w1(1, 1)
+        quantize_w1(2, 0)
+        open_products(1)
+        for g in range(PASSES):
+            product_pass(1, g)
+        open_products(2)
+        product_pass(2, 0)
+        cast_w1(2, 1)
         for c in range(1, CHUNKS):
             h[c] = sbuf("h%d" % c, [P, S], F32)
-        for c in (1, 2):
-            open_products(c)
-            product_pass(c, 0)
-        for c in (1, 2):
-            product_pass(c, 1)
-        open_sum(0, 0, HALF, 0)
-        open_sum(0, HALF, HALF, 2)
+        for piece in range(len(PIECES[1])):
+            gelu(1, piece)
         for g in range(PASSES):
             cast_w1(3, g)
-        take(0, 0, "w1_raw1_1")
-        for g in range(PASSES):
-            quantize_w1(3, g)
+        open_sum(0, 0, HALF, 0)
+        open_sum(0, HALF, HALF, 2)
+        take(0, 0, "w1_raw2_0")
+        quantize_w1(2, 1)
+        product_pass(2, 1)
+        open_sum(1, 0, HALF, 3)
+        open_sum(1, third, QUARTER, 4)
+        take(0, HALF, "w1_raw2_1")
+        quantize_w1(3, 0)
         open_products(3)
-        for g in range(PASSES):
-            product_pass(3, g)
-        for c in (1, 2):
-            for piece in range(len(PIECES[c])):
-                gelu(c, piece)
+        product_pass(3, 0)
+        taken_chunk1 = sbuf("w1_raw3_0", [P, HALF], F32)
+        gather_h(1, 0, taken_chunk1[:])
+        quantize_w1(3, 1)
+        product_pass(3, 1)
+        for piece in range(len(PIECES[2])):
+            gelu(2, piece)
         round_z(0, 0)
         for piece in range(len(PIECES[3])):
             gelu(3, piece)
-        take(0, HALF, "w1_raw3_1")
         round_z(0, HALF)
 
-        open_sum(1, 0, HALF, 3)
-        open_sum(1, third, QUARTER, 4)
-        take(1, 0, "taken_chunk1")
+        add_taken(1, 0, taken_chunk1[:])
         open_sum(2, 0, HALF, 5)
         open_sum(2, third, QUARTER, 6)
-        take(1, third, "taken_filler")
+        take(1, third, "w1_raw3_1")
         open_sum(1, fourth, QUARTER, 0, warm_up=HALF)
         round_z(1, 0)
         round_z(1, third)

@@ -179,15 +179,15 @@ def tile_picked_treeup_gelu_p_kernel(
         z_rows = sbuf("z_rows", [P, PACK * S], BF16)
         sums = {}
 
-        def open_sum(c, j0, width, number, warm_up=0):
+        def open_sum(c, j0, width, number, warm_up=()):
             whole = bank_tile(number, [P, HALF])
-            if warm_up:
+            for first, count in warm_up:
                 nc.tensor.matmul_mx(
-                    whole[:, 0:warm_up],
+                    whole[:, first : first + count],
                     lhsT=w2_codes[:].bitcast(FP8X4),
                     lhsT_scale=w2_plane[:],
-                    rhs=x_codes[0][:, 0:warm_up].bitcast(FP8X4),
-                    rhs_scale=x_plane[:, 0:warm_up],
+                    rhs=x_codes[0][:, first : first + count].bitcast(FP8X4),
+                    rhs_scale=x_plane[:, first : first + count],
                     start=True,
                     stop=True,
                 )
@@ -338,7 +338,7 @@ def tile_picked_treeup_gelu_p_kernel(
         open_sum(2, 0, HALF, 5)
         open_sum(2, third, QUARTER, 6)
         take(1, third, "w1_raw3_1")
-        open_sum(1, fourth, QUARTER, 0, warm_up=HALF)
+        open_sum(1, fourth, QUARTER, 0, warm_up=((0, QUARTER),))
         round_z(1, 0)
         round_z(1, third)
         take(2, 0, "stage0")
@@ -351,7 +351,7 @@ def tile_picked_treeup_gelu_p_kernel(
         take(3, QUARTER, "stage2")
         round_z(3, QUARTER)
 
-        open_sum(2, fourth, QUARTER, 4, warm_up=HALF)
+        open_sum(2, fourth, QUARTER, 4, warm_up=((0, QUARTER), (QUARTER, P)))
         take(2, third, "stage0")
         round_z(2, third)
         turn_back(0, 3)
@@ -360,7 +360,7 @@ def tile_picked_treeup_gelu_p_kernel(
         turn_back(1, 5)
         take(1, fourth, "stage2")
         round_z(1, fourth)
-        open_sum(3, fourth, P, 1, warm_up=HALF)
+        open_sum(3, fourth, P, 1, warm_up=((0, QUARTER),))
         open_sum(3, fourth + P, P, 7)
         take(2, fourth, "stage0")
         round_z(2, fourth)

@@ -32,7 +32,9 @@ PIECES = (
     ((0, HALF, 5), (HALF, HALF, 6)),
     ((0, HALF, 1), (HALF, HALF, 7)),
 )
-SPANS = {(0, 0): 1, (0, 1): 1, (1, 0): 1, (1, 1): 1, (2, 0): 1, (2, 1): 1, (3, 0): 1, (3, 1): 1}
+W1_TILES = [(c, g) for c in range(CHUNKS) for g in range(PASSES)]
+SHORT_WARM_UP = ((0, QUARTER),)
+LONG_WARM_UP = ((0, QUARTER), (QUARTER, P))
 STEPS = ((0, QUARTER), (QUARTER, QUARTER), (HALF, QUARTER), (HALF + QUARTER, P), (S - P, P))
 
 
@@ -61,8 +63,8 @@ def tile_picked_treeup_gelu_p_kernel(
         x_table = [sbuf("x_table%d" % g, [P, T], U32) for g in range(PASSES)]
         x_scale_table = sbuf("x_scale_table", [P, T], U8)
         w1_raw = {}
-        for first, g in SPANS:
-            w1_raw[first, g] = sbuf("w1_raw%d_%d" % (first, g), [P, PACK, P * SPANS[first, g]], F32)
+        for c, g in W1_TILES:
+            w1_raw[c, g] = sbuf("w1_raw%d_%d" % (c, g), [P, PACK, P], F32)
         share_sb = sbuf("share_sb", [P, S], F32)
         share_end = sbuf("share_end", [P, P], F32)
         share_cols = sbuf("share_cols", [P, S // P], F32)
@@ -80,11 +82,10 @@ def tile_picked_treeup_gelu_p_kernel(
             words = x_words[g].rearrange("p n t -> p (n t)").bitcast(I32)
             nc.sync.dma_start(out=x_table[g][:, lo:hi].bitcast(I32), in_=words[:, lo:hi])
 
-        def load_w1(first, g):
-            columns = slice(P * first, P * (first + SPANS[first, g]))
+        def load_w1(c, g):
             nc.sync.dma_start(
-                out=w1_raw[first, g][:],
-                in_=w1[PASS * g : PASS * (g + 1), columns].rearrange("(p r) m -> p r m", r=PACK),
+                out=w1_raw[c, g][:],
+                in_=w1[PASS * g : PASS * (g + 1), P * c : P * (c + 1)].rearrange("(p r) m -> p r m", r=PACK),
             )
 
         nc.sync.dma_start(offs_sb[:], offs)
@@ -96,16 +97,13 @@ def tile_picked_treeup_gelu_p_kernel(
                 in_=x_scales[:, 4 * quad : 4 * quad + 4, :].bitcast(I32),
             )
         load_x(0, T // 4, T)
-        load_w1(0, 0)
-        load_w1(0, 1)
+        for g in range(PASSES):
+            load_w1(0, g)
         load_x(1, 0, T)
         nc.sync.dma_start(par_sb[:], par)
-        load_w1(1, 0)
-        load_w1(1, 1)
-        load_w1(2, 0)
-        load_w1(2, 1)
-        load_w1(3, 0)
-        load_w1(3, 1)
+        for c in range(1, CHUNKS):
+            for g in range(PASSES):
+                load_w1(c, g)
         make_identity(nc, ident[:])
         nc.gpsimd.memset(w2_plane[:], 0)
         nc.sync.dma_start(out=w2_codes[:].bitcast(I32), in_=w2_words[0].rearrange("p n t -> p (n t)").bitcast(I32))
@@ -124,33 +122,25 @@ def tile_picked_treeup_gelu_p_kernel(
         w1_bf = {}
         w1_codes = {}
         w1_plane = {}
-        for first, g in SPANS:
-            count = SPANS[first, g]
-            w1_bf[first, g] = sbuf("w1_bf%d_%d" % (first, g), [P, P * count * PACK], BF16)
-            w1_codes[first, g] = sbuf("w1_codes%d_%d" % (first, g), [P, P * count], U32)
-            w1_plane[first, g] = sbuf("w1_plane%d_%d" % (first, g), [P, P * count], U8)
+        chunk_codes = {}
+        chunk_plane = {}
+        for c, g in W1_TILES:
+            w1_bf[c, g] = sbuf("w1_bf%d_%d" % (c, g), [P, P * PACK], BF16)
+            if g == 0:
+                chunk_codes[c] = sbuf("w1_codes%d" % c, [P, PASSES * P], U32)
+                chunk_plane[c] = sbuf("w1_plane%d" % c, [P, PASSES * P], U8)
+            w1_codes[c, g] = chunk_codes[c][:, P * g : P * (g + 1)]
+            w1_plane[c, g] = chunk_plane[c][:, P * g : P * (g + 1)]
 
-        def span_of(c, g):
-            first = c if (c, g) in SPANS else c - 1
-            return first, P * (c - first)
-
-        def cast_w1(c, g, on_scalar=True, chunks=1):
-            first, m0 = span_of(c, g)
-            m1 = m0 + P * chunks
+        def cast_w1(c, g, on_scalar=True):
             copy(
                 on_scalar,
-                w1_bf[first, g][:, PACK * m0 : PACK * m1].rearrange("p (m n r) -> p m r n", n=4, r=PACK),
-                w1_raw[first, g][:, :, m0:m1].rearrange("p r (m n) -> p m r n", n=4),
+                w1_bf[c, g][:].rearrange("p (m n r) -> p m r n", n=4, r=PACK),
+                w1_raw[c, g][:].rearrange("p r (m n) -> p m r n", n=4),
             )
 
-        def quantize_w1(c, g, chunks=1):
-            first, m0 = span_of(c, g)
-            m1 = m0 + P * chunks
-            nc.vector.quantize_mx(
-                out=w1_codes[first, g][:, m0:m1].bitcast(FP8X4),
-                scales=w1_plane[first, g][:, m0:m1],
-                in_=w1_bf[first, g][:, PACK * m0 : PACK * m1],
-            )
+        def quantize_w1(c, g):
+            nc.vector.quantize_mx(out=w1_codes[c, g].bitcast(FP8X4), scales=w1_plane[c, g], in_=w1_bf[c, g][:])
 
         x_codes = {}
         h = {}
@@ -159,13 +149,12 @@ def tile_picked_treeup_gelu_p_kernel(
         def open_products(c):
             products[c] = [(j0, width, bank_tile(number, [P, width])) for j0, width, number in PIECES[c]]
 
-        def product_pass(c, g, pieces=slice(None)):
-            first, m0 = span_of(c, g)
-            for j0, width, bank in products[c][pieces]:
+        def product_pass(c, g):
+            for j0, width, bank in products[c]:
                 nc.tensor.matmul_mx(
                     bank[:],
-                    lhsT=w1_codes[first, g][:, m0 : m0 + P].bitcast(FP8X4),
-                    lhsT_scale=w1_plane[first, g][:, m0 : m0 + P],
+                    lhsT=w1_codes[c, g].bitcast(FP8X4),
+                    lhsT_scale=w1_plane[c, g],
                     rhs=x_codes[g][:, j0 : j0 + width].bitcast(FP8X4),
                     rhs_scale=x_plane[4 * g : P, j0 : j0 + width],
                     start=(g == 0),
@@ -186,8 +175,8 @@ def tile_picked_treeup_gelu_p_kernel(
                     whole[:, first : first + count],
                     lhsT=w2_codes[:].bitcast(FP8X4),
                     lhsT_scale=w2_plane[:],
-                    rhs=x_codes[0][:, first : first + count].bitcast(FP8X4),
-                    rhs_scale=x_plane[:, first : first + count],
+                    rhs=chunk_codes[1][:, 0:count].bitcast(FP8X4),
+                    rhs_scale=chunk_plane[1][:, 0:count],
                     start=True,
                     stop=True,
                 )
@@ -214,18 +203,16 @@ def tile_picked_treeup_gelu_p_kernel(
             gather_h(c, j0, taken[:])
             add_taken(c, j0, taken[:])
 
-        def round_z(c, j0, on_scalar=True):
+        def round_z(c, j0):
             width, bank = sums[c, j0]
             rows = z_rows[:].rearrange("j (b u p e) -> j b u p e", u=2, p=P, e=2)
-            copy(
-                on_scalar,
+            nc.scalar.copy(
                 rows[:, j0 // P : (j0 + width) // P, :, 32 * c : 32 * (c + 1), :],
                 bank[:, 0 : width // P, :].rearrange("j b (p u e) -> j b u p e", u=2, e=2),
             )
 
         z_bf = {}
         acc = {}
-        late = {}
 
         def turn_back(step, number, on_scalar=True):
             j0, width = STEPS[step]
@@ -248,7 +235,7 @@ def tile_picked_treeup_gelu_p_kernel(
 
         def second_layer(step, number):
             j0, width = STEPS[step]
-            codes = late["z_codes"][:, j0 : j0 + width].bitcast(FP8X4)
+            codes = z_codes[:, j0 : j0 + width].bitcast(FP8X4)
             plane = z_plane[:, j0 : j0 + width]
             nc.vector.quantize_mx(out=codes, scales=plane, in_=z_bf[step][:])
             acc[step] = bank_tile(number, [P, width])
@@ -338,7 +325,7 @@ def tile_picked_treeup_gelu_p_kernel(
         open_sum(2, 0, HALF, 5)
         open_sum(2, third, QUARTER, 6)
         take(1, third, "w1_raw3_1")
-        open_sum(1, fourth, QUARTER, 0, warm_up=((0, QUARTER),))
+        open_sum(1, fourth, QUARTER, 0, warm_up=SHORT_WARM_UP)
         round_z(1, 0)
         round_z(1, third)
         take(2, 0, "stage0")
@@ -351,7 +338,7 @@ def tile_picked_treeup_gelu_p_kernel(
         take(3, QUARTER, "stage2")
         round_z(3, QUARTER)
 
-        open_sum(2, fourth, QUARTER, 4, warm_up=((0, QUARTER), (QUARTER, P)))
+        open_sum(2, fourth, QUARTER, 4, warm_up=LONG_WARM_UP)
         take(2, third, "stage0")
         round_z(2, third)
         turn_back(0, 3)
@@ -360,7 +347,7 @@ def tile_picked_treeup_gelu_p_kernel(
         turn_back(1, 5)
         take(1, fourth, "stage2")
         round_z(1, fourth)
-        open_sum(3, fourth, P, 1, warm_up=((0, QUARTER),))
+        open_sum(3, fourth, P, 1, warm_up=SHORT_WARM_UP)
         open_sum(3, fourth + P, P, 7)
         take(2, fourth, "stage0")
         round_z(2, fourth)
@@ -369,7 +356,7 @@ def tile_picked_treeup_gelu_p_kernel(
         for b in range(2):
             gather_h(3, fourth + P * b, taken_last[:, P * b : P * (b + 1)])
             add_taken(3, fourth + P * b, taken_last[:, P * b : P * (b + 1)])
-        late["z_codes"] = sbuf("share_sb", [P, S], U32)
+        z_codes = sbuf("share_sb", [P, S], U32)
         for b in range(2):
             round_z(3, fourth + P * b)
         second_layer(0, 2)

from contextlib import ExitStack

import concourse.mybir as mybir
from concourse.masks import make_identity

K, T, S, H, N = 1024, 2048, 1024, 512, 128
FLOPS = 2 * K * H * S + 2 * H * N * S

F32 = mybir.dt.float32
BF16 = mybir.dt.bfloat16
I32 = mybir.dt.int32
U32 = mybir.dt.uint32
U16 = mybir.dt.uint16
U8 = mybir.dt.uint8
FP8X4 = mybir.dt.float8_e4m3fn_x4
GELU = mybir.ActivationFunctionType.Gelu_apprx_tanh
MULT = mybir.AluOpType.mult

P = 128
PACK = 4
PASS = P * PACK
PASSES = K // PASS
CHUNKS = H // P
QUADRANTS = 4
LIST_ROWS = 16
HALF = S // 2
QUARTER = S // 4

PIECES = (
    ((0, HALF, 0), (HALF, QUARTER, 1), (HALF + QUARTER, QUARTER, 7)),
    ((0, HALF, 3), (HALF, HALF, 4)),
    ((0, HALF, 5), (HALF, HALF, 6)),
    ((0, HALF, 1), (HALF, HALF, 7)),
)
W1_TILES = [(c, g) for c in range(CHUNKS) for g in range(PASSES)]
SHORT_WARM_UP = ((0, QUARTER),)
LONG_WARM_UP = ((0, QUARTER), (QUARTER, P))
STEPS = ((0, QUARTER), (QUARTER, QUARTER), (HALF, QUARTER), (HALF + QUARTER, P), (S - P, P))


def tile_picked_treeup_gelu_p_kernel(
    tc, x_words, x_scales, w1, w2_words, w2_scales, share, offs, par, out
):
    nc = tc.nc
    with ExitStack() as ctx:
        keep = ctx.enter_context(tc.tile_pool(name="keep", bufs=1))
        psum = ctx.enter_context(tc.psum_pool(name="psum", bufs=1))

        def bank_tile(number, shape):
            return psum.tile(shape, F32, name="bank", tag="bank%d" % number)

        def sbuf(tag, shape, dtype):
            return keep.tile(shape, dtype, name=tag, tag=tag, align_bytes=64)

        def copy(on_scalar, dst, src):
            if on_scalar:
                nc.scalar.copy(dst, src)
            else:
                nc.vector.tensor_copy(dst, src)

        offs_sb = keep.tile([P, S // LIST_ROWS], U16, name="offs_sb")
        par_sb = keep.tile([P, S // LIST_ROWS], U16, name="par_sb")
        x_table = [sbuf("x_table%d" % g, [P, T], U32) for g in range(PASSES)]
        x_scale_table = sbuf("x_scale_table", [P, T], U8)
        w1_raw = {}
        for c, g in W1_TILES:
            w1_raw[c, g] = sbuf("w1_raw%d_%d" % (c, g), [P, PACK, P], F32)
        share_sb = sbuf("share_sb", [P, S], F32)
        share_end = sbuf("share_end", [P, P], F32)
        share_cols = sbuf("share_cols", [P, S // P], F32)
        w2_codes = sbuf("w2_codes", [P, N], U32)
        w2_plane = sbuf("w2_plane", [P, N], U8)
        ident = sbuf("ident", [P, P], F32)

        nc.gpsimd.memset(x_scale_table[:].bitcast(I32), 0)
        warm_in = sbuf("warm_in", [P, 1], F32)
        warm_out = sbuf("warm_out", [P, 1], F32)
        nc.vector.memset(warm_in[:], 0.0)
        nc.scalar.activation(warm_out[:], warm_in[:], GELU)

        def load_x(g, lo, hi):
            words = x_words[g].rearrange("p n t -> p (n t)").bitcast(I32)
            nc.sync.dma_start(out=x_table[g][:, lo:hi].bitcast(I32), in_=words[:, lo:hi])

        def load_w1(c, g):
            nc.sync.dma_start(
                out=w1_raw[c, g][:],
                in_=w1[PASS * g : PASS * (g + 1), P * c : P * (c + 1)].rearrange("(p r) m -> p r m", r=PACK),
            )

        nc.sync.dma_start(offs_sb[:], offs)
        nc.sync.dma_start(out=share_cols[:], in_=share[0].rearrange("(p b) -> p b", p=P))
        load_x(0, 0, T // 4)
        for quad in range(QUADRANTS):
            nc.sync.dma_start(
                out=x_scale_table[32 * quad : 32 * quad + 4 * PASSES, :].bitcast(I32),
                in_=x_scales[:, 4 * quad : 4 * quad + 4, :].bitcast(I32),
            )
        load_x(0, T // 4, T)
        for g in range(PASSES):
            load_w1(0, g)
        load_x(1, 0, T)
        nc.sync.dma_start(par_sb[:], par)
        for c in range(1, CHUNKS):
            for g in range(PASSES):
                load_w1(c, g)
        make_identity(nc, ident[:])
        nc.gpsimd.memset(w2_plane[:], 0)
        nc.sync.dma_start(out=w2_codes[:].bitcast(I32), in_=w2_words[0].rearrange("p n t -> p (n t)").bitcast(I32))
        for quad in range(QUADRANTS):
            nc.sync.dma_start(
                out=w2_plane[32 * quad : 32 * quad + 4, :].bitcast(I32),
                in_=w2_scales[0, 4 * quad : 4 * quad + 4, :].bitcast(I32),
            )

        def list_slice(list_sb, first, count):
            return list_sb[:, first // LIST_ROWS : (first + count) // LIST_ROWS]

        def gather_x(g, j0, width):
            nc.vector.tensor_copy(x_codes[g][:, j0 : j0 + width], x_table[g][:].indirect(list_slice(offs_sb, j0, width)))

        w1_bf = {}
        w1_codes = {}
        w1_plane = {}
        chunk_codes = {}
        chunk_plane = {}
        for c, g in W1_TILES:
            w1_bf[c, g] = sbuf("w1_bf%d_%d" % (c, g), [P, P * PACK], BF16)
            if g == 0:
                chunk_codes[c] = sbuf("w1_codes%d" % c, [P, PASSES * P], U32)
                chunk_plane[c] = sbuf("w1_plane%d" % c, [P, PASSES * P], U8)
            w1_codes[c, g] = chunk_codes[c][:, P * g : P * (g + 1)]
            w1_plane[c, g] = chunk_plane[c][:, P * g : P * (g + 1)]

        def cast_w1(c, g, on_scalar=True):
            copy(
                on_scalar,
                w1_bf[c, g][:].rearrange("p (m n r) -> p m r n", n=4, r=PACK),
                w1_raw[c, g][:].rearrange("p r (m n) -> p m r n", n=4),
            )

        def quantize_w1(c, g):
            nc.vector.quantize_mx(out=w1_codes[c, g].bitcast(FP8X4), scales=w1_plane[c, g], in_=w1_bf[c, g][:])

        x_codes = {}
        h = {}
        products = {}

        def open_products(c):
            products[c] = [(j0, width, bank_tile(number, [P, width])) for j0, width, number in PIECES[c]]

        def product_pass(c, g):
            for j0, width, bank in products[c]:
                nc.tensor.matmul_mx(
                    bank[:],
                    lhsT=w1_codes[c, g].bitcast(FP8X4),
                    lhsT_scale=w1_plane[c, g],
                    rhs=x_codes[g][:, j0 : j0 + width].bitcast(FP8X4),
                    rhs_scale=x_plane[4 * g : P, j0 : j0 + width],
                    start=(g == 0),
                    stop=(g == PASSES - 1),
                )

        def gelu(c, piece):
            j0, width, bank = products[c][piece]
            nc.scalar.activation(h[c][:, j0 : j0 + width], bank[:], GELU)

        z_rows = sbuf("z_rows", [P, PACK * S], BF16)
        sums = {}

        def open_sum(c, j0, width, number, warm_up=()):
            whole = bank_tile(number, [P, HALF])
            for first, count in warm_up:
                nc.tensor.matmul_mx(
                    whole[:, first : first + count],
                    lhsT=w2_codes[:].bitcast(FP8X4),
                    lhsT_scale=w2_plane[:],
                    rhs=chunk_codes[1][:, 0:count].bitcast(FP8X4),
                    rhs_scale=chunk_plane[1][:, 0:count],
                    start=True,
                    stop=True,
                )
            bank = whole[:].rearrange("j (b i) -> j b i", i=P)
            sums[c, j0] = (width, bank)
            for b in range(width // P):
                src = h[c][:, j0 + P * b : j0 + P * (b + 1)]
                nc.tensor.matmul(bank[:, b, :], lhsT=src, rhs=ident[:], is_transpose=True, start=(b == 0), stop=False)

        def gather_h(c, j0, taken):
            width = sums[c, j0][0]
            factor = share_end[:] if (j0, width) == (S - P, P) else share_sb[:, j0 : j0 + width]
            nc.vector.tensor_tensor(taken, h[c][:].indirect(list_slice(par_sb, j0, width)), factor, MULT)

        def add_taken(c, j0, taken):
            width, bank = sums[c, j0]
            blocks = width // P
            for b in range(blocks):
                src = taken[:, P * b : P * (b + 1)]
                nc.tensor.matmul(bank[:, b, :], lhsT=src, rhs=ident[:], is_transpose=True, start=False, stop=(b == blocks - 1))

        def take(c, j0, tag):
            taken = sbuf(tag, [P, sums[c, j0][0]], F32)
            gather_h(c, j0, taken[:])
            add_taken(c, j0, taken[:])

        def round_z(c, j0):
            width, bank = sums[c, j0]
            rows = z_rows[:].rearrange("j (b u p e) -> j b u p e", u=2, p=P, e=2)
            nc.scalar.copy(
                rows[:, j0 // P : (j0 + width) // P, :, 32 * c : 32 * (c + 1), :],
                bank[:, 0 : width // P, :].rearrange("j b (p u e) -> j b u p e", u=2, e=2),
            )

        z_bf = {}
        acc = {}

        def turn_back(step, number, on_scalar=True):
            j0, width = STEPS[step]
            pairs = z_rows[:].bitcast(F32)
            blocks = width // P
            whole = bank_tile(number, [P, HALF])
            bank = whole[:, 0 : 2 * width].rearrange("p (b u j) -> p b u j", u=2, j=P)
            for b in range(blocks):
                for u in range(2):
                    word0 = 2 * (j0 + P * b) + P * u
                    nc.tensor.transpose(bank[:, b, u, :], pairs[:, word0 : word0 + P], ident[:])
            z_bf[step] = sbuf("z_bf%d" % step, [P, PACK * width], BF16)
            copy(
                on_scalar,
                z_bf[step][:].bitcast(F32).rearrange("p (b j u) -> p b j u", b=blocks, u=2),
                bank.rearrange("p b u j -> p b j u"),
            )

        z_plane = sbuf("z_plane", [P, S], U8)

        def second_layer(step, number):
            j0, width = STEPS[step]
            codes = z_codes[:, j0 : j0 + width].bitcast(FP8X4)
            plane = z_plane[:, j0 : j0 + width]
            nc.vector.quantize_mx(out=codes, scales=plane, in_=z_bf[step][:])
            acc[step] = bank_tile(number, [P, width])
            nc.tensor.matmul_mx(
                acc[step][:],
                lhsT=w2_codes[:].bitcast(FP8X4),
                lhsT_scale=w2_plane[:],
                rhs=codes,
                rhs_scale=plane,
                start=True,
                stop=True,
            )

        def store(step, on_scalar=True):
            j0, width = STEPS[step]
            result = sbuf("result%d" % step, [P, width], F32)
            copy(on_scalar, result[:], acc[step][:])
            nc.sync.dma_start(out=out[:, j0 : j0 + width], in_=result[:])

        x_plane = sbuf("x_plane", [P, S], U8)
        nc.vector.tensor_copy(x_plane[:], x_scale_table[:].indirect(offs_sb[:]))
        x_codes[0] = sbuf("x_codes0", [P, S], U32)
        gather_x(0, 0, S)
        for g in range(PASSES):
            cast_w1(0, g)
            quantize_w1(0, g)
        for a in range(2):
            bank = bank_tile(6 + a, [P, 4, P])
            for b in range(4):
                nc.tensor.transpose(bank[:, b, :], share_cols[:, 4 * a + b : 4 * a + b + 1].to_broadcast([P, P]), ident[:])
            nc.scalar.copy(
                share_sb[:].rearrange("m (n b) -> m n b", n=P)[:, :, 4 * a : 4 * a + 4], bank[:].rearrange("m b n -> m n b")
            )
        nc.scalar.copy(share_end[:], share_sb[:, S - P : S])
        x_codes[1] = sbuf("x_codes1", [P, S], U32)
        for j0, width, number in PIECES[0]:
            gather_x(1, j0, width)
        for g in range(PASSES):
            cast_w1(1, g)
        open_products(0)
        for g in range(PASSES):
            product_pass(0, g)
        h[0] = sbuf("w1_raw1_0", [P, S], F32)
        for piece in range(len(PIECES[0])):
            gelu(0, piece)

        third, fourth = HALF, HALF + QUARTER
        quantize_w1(1, 0)
        cast_w1(2, 0, on_scalar=False)
        quantize_w1(1, 1)
        quantize_w1(2, 0)
        open_products(1)
        for g in range(PASSES):
            product_pass(1, g)
        open_products(2)
        product_pass(2, 0)
        cast_w1(2, 1)
        for c in range(1, CHUNKS):
            h[c] = sbuf("h%d" % c, [P, S], F32)
        for piece in range(len(PIECES[1])):
            gelu(1, piece)
        for g in range(PASSES):
            cast_w1(3, g)
        open_sum(0, 0, HALF, 0)
        open_sum(0, HALF, HALF, 2)
        take(0, 0, "w1_raw2_0")
        quantize_w1(2, 1)
        product_pass(2, 1)
        open_sum(1, 0, HALF, 3)
        open_sum(1, third, QUARTER, 4)
        take(0, HALF, "w1_raw2_1")
        quantize_w1(3, 0)
        open_products(3)
        product_pass(3, 0)
        taken_chunk1 = sbuf("w1_raw3_0", [P, HALF], F32)
        gather_h(1, 0, taken_chunk1[:])
        quantize_w1(3, 1)
        product_pass(3, 1)
        for piece in range(len(PIECES[2])):
            gelu(2, piece)
        round_z(0, 0)
        for piece in range(len(PIECES[3])):
            gelu(3, piece)
        round_z(0, HALF)

        add_taken(1, 0, taken_chunk1[:])
        open_sum(2, 0, HALF, 5)
        open_sum(2, third, QUARTER, 6)
        take(1, third, "w1_raw3_1")
        open_sum(1, fourth, QUARTER, 0, warm_up=SHORT_WARM_UP)
        round_z(1, 0)
        round_z(1, third)
        take(2, 0, "stage0")
        open_sum(3, 0, QUARTER, 1)
        open_sum(3, QUARTER, QUARTER, 7)
        round_z(2, 0)
        take(3, 0, "stage1")
        round_z(3, 0)
        open_sum(3, third, QUARTER, 2)
        take(3, QUARTER, "stage2")
        round_z(3, QUARTER)

        open_sum(2, fourth, QUARTER, 4, warm_up=LONG_WARM_UP)
        take(2, third, "stage0")
        round_z(2, third)
        turn_back(0, 3)
        take(3, third, "stage1")
        round_z(3, third)
        turn_back(1, 5)
        take(1, fourth, "stage2")
        round_z(1, fourth)
        open_sum(3, fourth, P, 1, warm_up=SHORT_WARM_UP)
        open_sum(3, fourth + P, P, 7)
        take(2, fourth, "stage0")
        round_z(2, fourth)
        turn_back(2, 6, on_scalar=False)
        taken_last = sbuf("stage1", [P, QUARTER], F32)
        for b in range(2):
            gather_h(3, fourth + P * b, taken_last[:, P * b : P * (b + 1)])
            add_taken(3, fourth + P * b, taken_last[:, P * b : P * (b + 1)])
        z_codes = sbuf("share_sb", [P, S], U32)
        for b in range(2):
            round_z(3, fourth + P * b)
        second_layer(0, 2)
        store(0)
        turn_back(3, 3)
        turn_back(4, 5)
        second_layer(1, 7)
        store(1)
        second_layer(2, 0)
        second_layer(3, 4)
        second_layer(4, 1)
        store(2)
        store(3, on_scalar=False)
        store(4)
